import numpy as np, ml_dtypes
CORES = [51,54,179,182]
N = 4
BF = ml_dtypes.bfloat16
def gentries(a):
    return np.ascontiguousarray(a.reshape(8, 16, -1).transpose(0, 2, 1)).reshape(8, -1)
def gtable(e):
    e = np.asarray(e); return np.ascontiguousarray(e.reshape(8, -1, 16).transpose(0, 2, 1)).reshape(128, -1).astype(np.int32)
NW, E, EP, C, U = 2048, 192, 3, 6, 2
def at(a, d):
    return np.roll(a, -1, axis=0) if d == 2 else a
def pick(a, ix):
    return np.take_along_axis(a, ix.reshape(8, 1, -1), 2).reshape(8, 16, E, 16)
def children(L, last, st, b):
    n = np.where(st, np.minimum(C, 15 - last), 0); end = np.add.accumulate(n, axis=-1); m = np.arange(16)
    k = np.add.reduce((end[..., None, :] <= m[:, None]).astype(np.int64), axis=-1)
    real = k < 16; k = np.minimum(k, 15)
    bb = np.where(real, np.take_along_axis(last, k, 2) + 1 + m - np.take_along_axis(end - n, k, 2), 15)
    Lk = np.take_along_axis(L, k, 2); Bb = np.take_along_axis(b, bb, 2)
    return np.where(real, (((Lk * Bb) >> 5) + Lk + 37 * Bb) & (NW - 1), NW - 1), bb, k
def grow(w, tau, b):
    names, par, votes = [[], [], []], [[], [], []], []
    for r in range(N):
        L = b[r]; last = np.zeros((8, E, 16), np.int64) + np.arange(16); p = np.zeros((8, E, 16), np.int64); c = np.zeros((8, E), np.int64)
        for d in range(3):
            q = (r + d) % N
            st = np.count_nonzero(pick(at(w[q], d), L) >= at(tau[q], d)[:, :, None, d:d + 1], axis=1) >= 9
            c = c + np.count_nonzero(st, axis=-1); names[d].append(L); par[d].append(p)
            if d < 2: L, last, p = children(L, last, st, b[r])
        votes.append(c)
    return names, par, np.stack(votes)
def winnow(w, names, fp, fn):
    new = []
    for q in range(N):
        bad = np.zeros((8, NW), bool); miss = np.zeros((8, NW), bool)
        for d in range(3):
            r = (q - d) % N; ix = names[d][r][:, :, :U]
            h = np.zeros(ix.shape, np.int64) + ((np.arange(8) + (d == 2)) % 8)[:, None, None]
            for flag, hit in ((fp, bad), (fn, miss)):
                on = np.zeros(ix.shape, bool) | flag[r][:, :, None]
                hit[h[on], ix[on]] = True
        fac = np.where(miss, 2.0, np.where(bad, 0.5, 1.0)).astype(np.float32)
        v = np.minimum(np.maximum(w[q] * fac[:, None, :], np.float32(0.25)), np.float32(4.0)); v[:, :, NW - 1] = 0
        new.append(v)
    return np.stack(new)
def bf(a):
    return np.asarray(a).astype(BF).astype(np.float32)
def parts(rng, off=0.8):
    f = 0.5 + 0.75 * rng.random((128, NW))
    t0 = bf(np.exp2(0.8 * rng.random((N, 8, 16, 3)) - 0.4)); up = rng.integers(0, 4, t0.shape)
    tau = np.where(up < 2, t0, np.where(up == 2, t0 * np.float32(1.0 + 2.0 ** -12), np.nextafter(t0, np.float32(8.0)))).astype(np.float32)
    z = off * (2.0 * rng.random((N, 8, 1, 1), dtype=np.float32) - 1.0) + 3.2 * rng.random((N, 8, 1, NW), dtype=np.float32) - 1.6 + 1.2 * rng.random((N, 8, 16, NW), dtype=np.float32) - 0.6
    w = np.where(rng.random((N, 8, 16, NW), dtype=np.float32) < 0.1, np.take_along_axis(t0, rng.integers(0, 3, (N, 8, 1, NW)), 3), np.exp2(z))
    w = bf(np.minimum(np.maximum(w, 0.25), 4.0)); w[..., NW - 1] = 0
    b = rng.integers(0, NW - 1, (EP, N, 8, E, 16))
    x = 0.5 + 0.5 * rng.random((N, 128, EP * E))
    return f, w, b, x, tau
def tune(rng, w, tau, b, codes, share):
    lab, ask = [], []; codes = np.broadcast_to(codes, (EP - 1, N, 8, E))
    for t in range(EP - 1):
        names, par, c = grow(w, tau, b[t]); code = codes[t]
        near = c + rng.integers(0, 2, c.shape)
        loose = np.where(rng.random(c.shape) < 0.7, c + rng.integers(-2, 4, c.shape), rng.integers(1, 49, c.shape))
        ends = np.where(rng.random(c.shape) < 0.7, rng.choice(np.array([1, 48]), c.shape), near)
        a = np.where(code == 0, loose, np.where(code == 1, c, np.where(code == 2, c + 1, np.where(code == 3, near, ends))))
        a = np.minimum(np.maximum(a, 1), 48)
        y = np.where((code == 1) | (code == 3), 0, np.where(code == 2, 1, (rng.random(c.shape) < share).astype(np.int64)))
        lab.append(y); ask.append(a)
        if t < EP - 2: w = winnow(w, names, (c >= a) & (y == 0), (c < a) & (y == 1))
    return np.stack(lab), np.stack(ask)
def pack(rng, f, w, b, x, tau, code, share):
    lab, ask = tune(rng, w, tau, b, code, share)
    f = np.array(f); f[:, NW - 1] = 0
    flat = lambda a: np.ascontiguousarray(a.transpose(1, 2, 0, 3).reshape(N, 8, -1)).astype(np.int32)
    return {"ft": np.stack([f.astype(BF)] * N), "wt": np.ascontiguousarray(w.reshape(N, 128, NW)).astype(BF),
            "bn": np.stack([gtable(b[:, r].transpose(1, 0, 2, 3).reshape(8, -1)) for r in range(N)]), "xv": x.astype(BF),
            "tau": np.ascontiguousarray(tau.reshape(N, 128, 3)).astype(np.float32), "lab": flat(lab), "ask": flat(ask)}
def setup_inputs(rng):
    f, w, b, x, tau = parts(rng)
    return pack(rng, f, w, b, x, tau, np.zeros((N, 8, E), np.int64), rng.choice(np.array([0.15, 0.3, 0.5]), (N, 8, 1)))
def setup_inputs_spread(rng):
    f, w, b, x, tau = parts(rng)
    x = x * np.exp2(rng.integers(-1, 2, (N, 1, EP * E)))
    b = np.minimum(((NW - 1) * rng.random(b.shape) ** 3).astype(np.int64), NW - 2)
    w = bf(np.exp2(4.0 * rng.random(w.shape, dtype=np.float32) - 2.0)); w[..., NW - 1] = 0
    return pack(rng, f, w, b, x, tau, np.zeros((N, 8, E), np.int64), rng.choice(np.array([0.05, 0.3, 0.6]), (N, 8, 1)))
def setup_inputs_ends(rng):
    f, w, b, x, tau = parts(rng)
    f = np.where(rng.random(f.shape) < 0.5, 0.5, 1.25); x = np.where(rng.random(x.shape) < 0.5, 0.25, 2.0)
    w = np.where(rng.random(w.shape) < rng.choice(np.array([0.0, 0.5, 1.0]), (N, 8, 1, NW)), 4.0, 0.25).astype(np.float32)
    w[:, 1, :, 0] = 0.25; w[:, 1, :, NW - 2] = 0.25; w[:, 6, :, 0] = 0.25; w[:, 6, :, NW - 2] = 0.25; w[..., NW - 1] = 0
    low = np.array([9, 0, 5, 6, 7, 8, 6, 16])[None, :, None, None]
    tau = np.where(np.argsort(rng.random((N, 8, 16, 3)), axis=2) < low, 0.25, 4.0).astype(np.float32)
    two = rng.choice(np.array([0, NW - 2]), b.shape); m = rng.random(b.shape) < 0.7; m[:, :, 1, ::2] = True; m[:, :, 6, ::2] = True
    b = np.where(m, two, b)
    return pack(rng, f, w, b, x, tau, np.full((N, 8, E), 4), np.array([0.5, 0.03, 0.97, 0.3, 0.5, 0.1, 0.9, 0.3])[None, :, None])
def pattern(T):
    on = np.zeros(16, bool)
    for k in range(15):
        n = min(C, 15 - k)
        if n <= T: on[k] = True; T = T - n
    return on
def setup_inputs_corners(rng):
    f, w, b, x, tau = parts(rng); tau[:, 1:] = 0.375; slot = np.arange(16); e = np.arange(E)[:, None]
    size = (0, NW - 1, NW - 2, NW - 2, 64, 64, 64, NW >> 1)
    pats = np.stack([pattern(T) for T in (0, 1, C, 15, 16, 17, 40)] + [slot >= 0, slot == 15])
    for r in range(N):
        for g in range(1, 8):
            o = rng.permutation(NW - 1); H = size[g]; m = np.zeros(NW, bool); m[o[:H]] = True
            w[r, g] = bf(np.where(m, 3.0 + rng.random((16, NW)), 0.25 + 0.05 * rng.random((16, NW))))
            for t in range(EP):
                if g == 1: want = np.ones((E, 16), bool)
                elif g < 4: want = (slot < 15) | ((e + t) % 2 == 0)
                elif g < 7: want = slot >= 16 - ((e + t + r) & 3)
                else: want = pats[(np.arange(E) + t) % len(pats)]
                b[t, r, g] = o[np.where(want, rng.integers(0, H, (E, 16)), rng.integers(min(H, NW - 2), NW - 1, (E, 16)))]
    w[..., NW - 1] = 0
    code = np.zeros((N, 8, E), np.int64); code[:, 0] = 2; code[:, 1:7] = 3
    return pack(rng, f, w, b, x, tau, code, np.full((N, 8, 1), 0.4))
def setup_inputs_crowd(rng):
    f, w, b, x, tau = parts(rng)
    b[:, :, :5] = 0
    for t in range(EP):
        for r in range(N): b[t, r, 4, int(rng.integers(0, E)), int(rng.integers(0, U))] = int(rng.integers(1, NW - 1))
    b[:, :, 5] = rng.choice(rng.integers(0, NW - 1, 3), (EP, N, E, 16)); b[:, :, 6] = int(rng.integers(1, NW - 1))
    w[:, :5, :, 0] = 1.0; tau[..., :2] = 0.3; tau[..., 2] = 3.0
    other = rng.integers(1, NW - 1, (EP, N)); w[:, 2:4, :, other.reshape(-1)] = 1.0
    code = np.zeros((N, 8, E), np.int64); code[:, :5] = 1; code[:, 6] = 2
    for r in range(N):
        e = int(rng.integers(0, E)); code[r, 2, e] = 2; b[:, r, 2, e, 0] = other[:, r]
        code[r, 4, int(rng.integers(0, E))] = 2
    return pack(rng, f, w, b, x, tau, code, np.full((N, 8, 1), 0.3))
def setup_inputs_full(rng):
    f, w, b, x, tau = parts(rng, 0.0); tau = np.nextafter(bf(tau), np.float32(8.0))
    b[..., :U] = np.argsort(rng.random((EP, N, 8, NW - 1)), axis=-1)[..., :E * U].reshape(EP, N, 8, E, U)
    return pack(rng, f, w, b, x, tau, np.where(np.arange(EP - 1) % 2 == 0, 2, 1)[:, None, None, None], np.full((N, 8, 1), 0.5))
def check_ranges(d):
    bad = []
    for k, lo, hi in (("bn", 0, NW - 2), ("lab", 0, 1), ("ask", 1, 48), ("tau", 0.25, 4)):
        v = np.asarray(d[k])
        if not np.all((v >= lo) & (v <= hi)): bad.append("range of " + k)
    for k, lo, hi in (("ft", 0.5, 1.25), ("wt", 0.25, 4)):
        v = np.asarray(d[k]).astype(np.float32)
        if not np.all((v[..., :NW - 1] >= lo) & (v[..., :NW - 1] <= hi)): bad.append("range of " + k)
        if not np.all(v[..., NW - 1] == 0): bad.append("last column of " + k)
    v = np.asarray(d["ft"]).astype(np.float32)
    if not np.all(v == v[:1]): bad.append("ft is not alike on all ranks")
    v = np.asarray(d["xv"]).astype(np.float32)
    if not np.all((v >= 0.25) & (v <= 2)): bad.append("range of xv")
    return bad
def reference(ft, wt, bn, xv, tau, lab, ask):
    f = np.asarray(ft).astype(np.float64).reshape(N, 8, 16, NW); w = np.asarray(wt).astype(np.float32).reshape(N, 8, 16, NW); ta = np.asarray(tau).astype(np.float32).reshape(N, 8, 16, 3)
    b = np.stack([gentries(a) for a in bn]).astype(np.int64).reshape(N, 8, EP, E, 16)
    la = np.asarray(lab).reshape(N, 8, EP - 1, E); need = np.asarray(ask).reshape(N, 8, EP - 1, E); ys, cs = [], []
    for t in range(EP):
        names, par, c = grow(w, ta, b[:, :, t]); s = np.zeros((N, 8, 16, E))
        for r in range(N):
            for d in range(3):
                q = (r + d) % N; L = names[d][r]; fl = pick(at(f[q], d), L)
                v = fl if d == 0 else np.take_along_axis(v, par[d][r][:, None], 3) * fl
                s[r] += np.add.reduce(v * pick(at(w[q], d), L), axis=3)
        ys.append(s); cs.append(c)
        if t < EP - 1:
            yes = c >= need[:, :, t]
            w = winnow(w, names, yes & (la[:, :, t] == 0), ~yes & (la[:, :, t] == 1))
    y = np.stack(ys).transpose(1, 2, 3, 0, 4).reshape(N, 128, EP * E) * np.asarray(xv).astype(np.float64)
    return {"y": y.astype(np.float32), "cv": np.stack(cs).transpose(1, 2, 0, 3).reshape(N, 8, EP * E).astype(np.float32)}

def check_inputs(d):
    bad = list(check_ranges(d))
    if not bad:
        for name, y in reference(**d).items():
            for q in range(N):
                v = np.abs(np.asarray(y[q], np.float64)); s = np.sqrt(np.mean(v * v))
                if v.max() > 8 * s or s < 2.0 ** 3: bad.append('%s of rank %d is uneven or too small' % (name, q))
    return bad

@@ -1,0 +1,758 @@
+import numpy as np
+from concourse.bass import DstId, RemoteDMATransfer
+from concourse.mybir import AluOpType as A, ActivationFunctionType as F
+
+NW, E, EP, HW = 2048, 192, 3, 64
+NP, W2, WIDE, NC = E // HW, 2 * HW, 16 * HW, HW // 16
+DW, SW = 17 * NC, 136 * NC
+ARENA = {"af": "float32", "ab": "bfloat16", "ah": "float16", "ai": "int32", "au": "uint16"}
+SIZE = {"af": 4, "ab": 2, "ah": 2, "ai": 4, "au": 2}
+TOP = {k: 0 for k in ARENA}
+OPS, SEMS = [], ["cV", "cS", "cP", "cG", "sent"]
+CY, PC = 0.92, 0.47
+RED = (0, 1, 2)
+RB = (3, 7, 7)
+SIGHT, GAP, GRAIN = 3000.0, 5000.0, 50.0
+VIAPE = True
+THV, ONV = (2,), ()
+SLACK, TURNS, MIX, CUT, PCUT = 300.0, 1, 3000.0, 2, 4
+HEAT, SEED, LEAD, UP = 300.0, 1, 1500.0, [0.0]
+
+
+def alloc(a, n):
+    c = TOP[a]
+    TOP[a] = c + (n + 15) // 16 * 16
+    return (a, 0, 128, 1, c, c + n, 1)
+
+
+def sub(v, a, b, s=1):
+    return v[:4] + (v[4] + a, v[4] + b, s)
+
+
+def part(v, a, b, s=1):
+    return (v[0], a, b, s) + v[4:]
+
+
+def bank(b, a, n):
+    return ("ps%d" % b, 0, 128, 1, a, a + n, 1)
+
+
+def pb(h, u, n=1, second=0):
+    return bank(2 * h + second if NP == 2 else h, u * HW, n * HW)
+
+
+def hbm(name, r0, r1, c0, c1):
+    return (name, r0, r1, 1, c0, c1, 1)
+
+
+def wid(v):
+    return (v[5] - v[4] + v[6] - 1) // v[6]
+
+
+def isv(x):
+    return isinstance(x, tuple)
+
+
+def ap(T, v):
+    if not isv(v):
+        return v
+    if v[0] == "ind":
+        return ap(T, v[1]).indirect(ap(T, v[2]))
+    return T[v[0]][v[1]:v[2]:v[3], v[4]:v[5]:v[6]]
+
+
+def ind(win, off):
+    return ("ind", win, off)
+
+
+def views(xs):
+    out = []
+    for x in xs:
+        if isv(x):
+            out += [x[1], x[2]] if x[0] == "ind" else [x]
+    return out
+
+
+def narrow(vs):
+    return all(SIZE.get(v[0], 4) == 2 for v in vs)
+
+
+def vcost(out, ins, rate):
+    if any(isv(x) and x[0] == "ind" for x in ins):
+        return 55 + wid(out) * 1.56 * CY
+    return 25 + max(64, wid(out) * rate) * CY
+
+
+def tt(out, a, b, op):
+    r = 1 if a[0][:2] == "ps" or b[0][:2] == "ps" else 2
+    return ("tensor_tensor", (out, a, b, op), {}, views([a, b]), [out], vcost(out, [a], r))
+
+
+def ts(out, a, s1, o1, s2=None, o2=None):
+    args = (out, a, s1, s2, o1) + (() if o2 is None else (o2,))
+    return ("tensor_scalar", args, {}, views([a, s1, s2]), [out], vcost(out, [a], 0.5 if narrow([out, a]) else 1))
+
+
+def cp(out, a):
+    return ("tensor_copy", (out, a), {}, views([a]), [out], vcost(out, [a], 0.5 if narrow([out, a]) else 1))
+
+
+def tr(out, a):
+    return ("transpose", (out, a), {}, [a], [out], vcost(out, [a], 0.5 if narrow([out, a]) else 1))
+
+
+def scan(out, a, b, init, o0, o1):
+    return ("tensor_tensor_scan", (out, a, b, init, o0, o1), {}, [a, b], [out], vcost(out, [a], 1))
+
+
+def fill(out, c):
+    return ("memset", (out, c), {}, [], [out], vcost(out, [], 0.5 if narrow([out]) else 1))
+
+
+def act(out, a, f, bias=None, scale=None):
+    kw = {} if bias is None else {"bias": bias}
+    if scale is not None:
+        kw["scale"] = scale
+    return ("activation", (out, a, f), kw, views([a, bias, scale]), [out], vcost(out, [a], 1) + 15)
+
+
+def mm(out, l, r, start=True, stop=True):
+    c = max(min(64, wid(l)), wid(r)) * (4 if l[0] == "af" else 1) * PC
+    return ("matmul", (out, l, r, start, stop), {}, [l, r], [out], c)
+
+
+def iota(out, pat, base, cm):
+    kw = {} if out[0] == "ai" else {"allow_small_or_imprecise_dtypes": True}
+    return ("iota", (out, pat, base, cm), kw, [], [out], 150 + 2 * CY * wid(out))
+
+
+def pick(out, a, pat, base, cm):
+    return ("affine_select", (out, a, pat, A.is_equal, 0.0, base, cm), {}, [a], [out], 190 + 2 * CY * wid(out))
+
+
+def emit(q, ins, kind="c", sem=None, extra=None, lat=0, late=0.0):
+    ins = ins if isinstance(ins, list) else [ins]
+    OPS.append({"q": q, "ins": ins, "kind": kind, "sem": sem, "x": extra, "lat": lat, "late": late, "up": UP[0],
+                "R": [v for i in ins for v in i[3]], "W": [v for i in ins for v in i[4]], "ns": sum(i[5] for i in ins)})
+
+
+def V(i):
+    emit("V", i)
+
+
+def S(i):
+    emit("S", i)
+
+
+def P(i):
+    emit("P", i)
+
+
+def group(out, pairs):
+    return [mm(out, l, r, j == 0, j == len(pairs) - 1) for j, (l, r) in enumerate(pairs)]
+
+
+def dma(q, pairs, lat, sem=None):
+    if sem is None:
+        sem = "d%d" % len(SEMS)
+    if sem not in SEMS:
+        SEMS.append(sem)
+    emit(q, [("dma_start", (o, i), {}, [i], [o], 60 if q != "G" else 900) for o, i in pairs], "d", sem, None, lat)
+
+
+def send(trs):
+    sem = "r%d" % len(SEMS)
+    SEMS.append(sem)
+    emit("G", [("send", (), {}, [s for s, d in trs], [l for s, d in trs for k, l in d], 600)], "r", sem, trs,
+         1500 + 800 * len(trs) * max(len(d) for s, d in trs))
+
+
+def plan():
+    f32 = lambda n: alloc("af", n)
+    b16 = lambda n: alloc("ab", n)
+    h16 = lambda n: alloc("ah", n)
+    i32 = lambda n: alloc("ai", n)
+    u16 = lambda n: alloc("au", n)
+    half = lambda v, h: sub(v, h * HW, (h + 1) * HW)
+
+    w, wU, ft, fR = b16(NW), b16(NW), b16(NW), b16(NW)
+    bn, tau, xv, al = i32(EP * E), f32(3), b16(EP * E), i32(4 * E)
+    dma("Y", [(w, hbm("wt", 0, 128, 0, NW))], 3200)
+    dma("S", [(tau, hbm("tau", 0, 128, 0, 3))], 1800)
+    dma("S", [(bn, hbm("bn", 0, 128, 0, EP * E))], 2400)
+    dma("Y", [(ft, hbm("ft", 0, 128, 0, NW))], 4500)
+    dma("Y", [(part(sub(al, 0, 2 * E), 0, 8), hbm("ask", 0, 8, 0, 2 * E)), (part(sub(al, 2 * E, 4 * E), 0, 8), hbm("lab", 0, 8, 0, 2 * E))], 3000)
+    dma("Y", [(part(fR, 16, 128), hbm("ft", 0, 112, 0, NW)), (part(fR, 0, 16), hbm("ft", 112, 128, 0, NW))], 6000)
+    dma("Y", [(xv, hbm("xv", 0, 128, 0, EP * E))], 6000)
+
+    CP, PI, EI = i32(E), i32(1), i32(E)
+    emit("G", iota(PI, [[1, 1]], 0, 1))
+    emit("G", iota(EI, [[1, E]], 0, 0))
+    emit("G", iota(CP, [[1, 128]], 0, -1) if False else iota(sub(CP, 0, 128), [[1, 128]], 0, -1))
+    mi, gi, mcol, gcol = i32(1), i32(1), f32(1), f32(1)
+    V(ts(mi, PI, 15, A.bitwise_and)); V(ts(gi, PI, 112, A.bitwise_and)); V(cp(mcol, mi)); V(cp(gcol, gi))
+    t160, u160 = i32(160), i32(160)
+    SELb, SELh, EXT, BW = b16(160), h16(160), b16(160), b16(160)
+    V(ts(t160, sub(EI, 0, 160), gcol, A.subtract, 96.0, A.add))
+    V(ts(u160, t160, 127, A.bitwise_and))
+    V(ts(SELb, u160, 0.0, A.is_equal)); V(cp(SELh, SELb))
+    sel = lambda M, s, roll=0: sub(M, 32 - s - 16 * roll, 160 - s - 16 * roll)
+    x0, x1 = f32(1), f32(1)
+    V(ts(x0, mcol, 0.0, A.is_equal, 32.0, A.mult)); V(ts(x1, mcol, 1.0, A.is_equal, x0, A.add))
+    S(act(EXT, SELb, F.Identity, None, x1))
+    t2, u2 = i32(160), i32(160)
+    V(ts(t2, t160, 16.0, A.add)); V(ts(u2, t2, 112, A.bitwise_and)); V(ts(BW, u2, 0.0, A.is_equal))
+    BLK, ROLL, UNROLL = sub(BW, 16, 144), sub(BW, 0, 128), sub(BW, 32, 160)
+    cp128 = sub(CP, 0, 128)
+    I1, I8, PI4, NI4, T256, T248, tri, IC, RF = b16(128), b16(128), b16(128), b16(128), b16(128), b16(128), b16(128), h16(128), f32(128)
+    V(ts(tri, cp128, 0.0, A.is_gt)); V(tt(tri, tri, BLK, A.mult))
+    V(ts(I1, cp128, 0.0, A.is_equal))
+    S([act(M, x, F.Copy, None, c) for M, x, c in ((T256, tri, -256.0), (T248, tri, -248.0))])
+    S([act(M, I1, F.Copy, None, c) for M, c in ((NI4, -4096.0), (PI4, 4096.0), (I8, 8.0))])
+    V(ts(IC, I1, -58.5, A.mult))
+    SEL256, TRI = h16(160), b16(128)
+    V(ts(SEL256, SELb, 256.0, A.mult))
+    V(tt(TRI, tri, I1, A.add))
+    rt, ru = i32(128), i32(128)
+    V(ts(rt, cp128, 144.0, A.add)); V(ts(ru, rt, 127, A.bitwise_and)); V(ts(RF, ru, 0.0, A.is_equal))
+    ONES = h16(HW); V(fill(ONES, 547.0))
+    bb1, nl1, zz1, E16 = b16(HW), b16(HW), b16(HW), f32(E)
+    V(ts(bb1, sub(EI, 0, HW), 0.0, A.mult, mcol, A.add)); V(ts(bb1, bb1, 16.0, A.add))
+    V(ts(nl1, bb1, 25.0, A.max, 31.0, A.subtract)); V(ts(zz1, bb1, 30.0, A.max, 29.5, A.subtract))
+    V([ts(half(E16, h), sub(EI, 0, HW), 16.0, A.mult, 8.0, A.add) for h in range(NP)])
+    SELq = b16(160)
+    S(act(SELq, SELb, F.Copy, None, 0.5))
+    nlc, m192, cap, mneg, m16, EM = f32(1), f32(1), f32(1), f32(1), f32(1), f32(E)
+    V(cp(nlc, sub(nl1, 0, 1)))
+    V(ts(m192, mcol, float(E), A.mult)); V(ts(cap, m192, -1.0, A.mult, 15.0 * E, A.add))
+    V(ts(mneg, mcol, -1.0, A.mult)); V(ts(m16, mcol, 16.0, A.add)); V(ts(EM, EI, m192, A.add))
+    YL, yl = u16(8), f32(8)
+    V(ts(yl, sub(EI, 0, 8), 17.0, A.mult, mcol, A.add)); V(cp(YL, yl))
+    a0, a1, a2, a3, nth = f32(3), i32(3), f32(3), f32(3), f32(3)
+    V(ts(a0, tau, 512.0, A.mult)); V(cp(a1, a0)); V(cp(a2, a1)); V(tt(a3, a2, a0, A.is_lt)); V(tt(a2, a2, a3, A.add))
+    V(ts(a3, a2, 128.0, A.is_equal, 96.0, A.mult)); V(tt(a2, a3, a2, A.subtract)); V(ts(nth, a2, 0.25, A.add, 1.0 / 512, A.mult))
+    L1 = u16(EP * E)
+    V(cp(sub(L1, 0, E), sub(bn, 0, E))); V(cp(sub(L1, E, EP * E), sub(bn, E, EP * E)))
+    HL, HLn, hi_, lo_ = b16(2 * EP * E), b16(2 * EP * E), i32(E), i32(E)
+    for t in range(EP):
+        V([ts(hi_, sub(bn, t * E, (t + 1) * E), 5, A.arith_shift_right), ts(lo_, sub(bn, t * E, (t + 1) * E), 31, A.bitwise_and)])
+        V([ts(sub(HL, 2 * t * E, (2 * t + 1) * E), hi_, 1.0, A.add), cp(sub(HL, (2 * t + 1) * E, (2 * t + 2) * E), lo_)])
+        if t != 1:
+            a = 0 if t == 0 else 2 * E
+            send([(sub(HL, a, (2 * t + 2) * E), [(1, sub(HLn, a, (2 * t + 2) * E))])])
+    WIN = [b16(16 * E), b16(16 * E)]
+    for j in range(2):
+        dma("Y", [(sub(WIN[j], 0, NW), hbm("ft", 0, 128, 0, NW)), (sub(WIN[j], NW, 16 * E), hbm("ft", 0, 128, 0, 16 * E - NW))], 5000)
+    IF = f32(128)
+    S(act(IF, I1, F.Copy))
+    NF, CT = f32(128), f32(HW)
+    S(act(NF, I1, F.Copy, None, -1.0)); V(fill(CT, -63328.5))
+    if VIAPE:
+        IS = f32(128)
+        S(act(IS, I1, F.Copy, None, E / 2048.0))
+    if len(RED) < 3:
+        SCB = f32(2 * SW + 8)
+        V(fill(sub(SCB, 7, 2 * SW + 8, 136), 0.0))
+    alb, REP, rp, VD, VDn = b16(4 * E), b16(128), i32(128), b16(6 * E), b16(6 * E)
+    emit("G", iota(part(rp, 0, 8), [[1, 128]], 0, -16))
+    V(ts(part(rp, 0, 8), part(rp, 0, 8), 4, A.arith_shift_right)); V(ts(part(REP, 0, 8), part(rp, 0, 8), 0.0, A.is_equal))
+    V(cp(part(alb, 0, 8), part(al, 0, 8)))
+    P(mm(bank(4, 0, 2 * E), part(REP, 0, 8), part(sub(alb, 0, 2 * E), 0, 8)))
+    P(mm(bank(5, 0, 2 * E), part(REP, 0, 8), part(sub(alb, 2 * E, 4 * E), 0, 8)))
+    S(act(sub(VD, 0, 2 * E), bank(4, 0, 2 * E), F.Copy)); S(act(sub(VD, 2 * E, 4 * E), bank(5, 0, 2 * E), F.Copy))
+    V(ts(sub(VD, 4 * E, 6 * E), sub(VD, 2 * E, 4 * E), -4095.0, A.mult, -1.0, A.add))
+    send([(VD, [(2, VDn)])])
+    EK, hc, E0R, HP, IO = b16(NW), f32(1), b16(128), b16(384), b16(128)
+    emit("G", iota(EK, [[0, NW]], 1, 0), late=7000.0)
+    emit("G", pick(EK, EK, [[-1, 16], [-16, 8], [0, 16]], 0, 1))
+    V(ts(hc, mcol, 0.0, A.is_equal)); V(ts(E0R, ROLL, hc, A.mult))
+    E8h, E8n = h16(16), b16(16)
+    V([cp(E8h, sub(EK, 0, 256, 16)), ts(E8n, sub(EK, 0, 256, 16), -128.0, A.mult)])
+    emit("G", iota(HP, [[0, 24], [1, 16]], 129, 0), late=7000.0)
+    emit("G", iota(IO, [[1, 128]], 0, 0), late=7000.0)
+    ek = lambda k: sub(EK, 128 * k, 128 * k + 128)
+
+    PT = [f32(NW), f32(NW)]
+    SG = BG = [b16(WIDE) for h in range(NP)]
+    YY = [h16(16 * W2) for h in range(NP)]
+    tv = [[f32(WIDE) for h in range(NP)] for d in range(2)]
+    v2 = [f32(WIDE + 16) for h in range(NP)]
+    V([fill(sub(v2[h], WIDE, WIDE + 16), 0.0) for h in range(NP)])
+    TH = b16(NP * WIDE)
+    av = [sub(TH, h * WIDE, (h + 1) * WIDE) for h in range(NP)]
+    HOT, A0, AW, LOC = b16(72 * 128), b16(1152), b16(1152), b16(72)
+    tmp = {}
+
+    def T_(name, h, mk, n):
+        if (name, h) not in tmp:
+            tmp[(name, h)] = mk(n)
+        return tmp[(name, h)]
+
+    M23, M34 = 1.5 * 2.0 ** 23, 1.5 * 2.0 ** 34
+
+    def products(t):
+        for c in range(4):
+            s = lambda v: sub(v, 512 * c, 512 * c + 512)
+            bk = bank((4, 5, 6, 4)[c], 0, 512)
+            P(mm(bk, I1, s(w)))
+            V(tt(s(PT[t % 2]), bk, s(ft), A.mult))
+
+    def windows(t, j):
+        for k in range(2):
+            src = sub(HLn if j else HL, (2 * t + k) * E, (2 * t + k + 1) * E)
+            if j:
+                dma("Y", [(part(WIN[1], 16 + k, 128, 16), part(src, 0, 112)), (part(WIN[1], k, k + 1), part(src, 112, 128))], 2500)
+            else:
+                dma("Y", [(part(WIN[0], k, 128, 16), src)], 2500)
+
+    def strong(t, d, h, lst):
+        S(act(SG[h], ind(w if t == 0 else wU, lst), F.Sign, sub(nth, d, d + 1)))
+        cnt = pb(h, 0)
+        P(group(cnt, [(sel(SELb, k), sub(SG[h], k, WIDE, 16)) for k in range(16)]))
+        return cnt
+
+    def children(t, d, h, cnt, st, pay, bb, nl, zz, oL, oP, obb):
+        n = T_("n%d" % d, h, b16, HW)
+        V(ts(st, cnt, 1.0, A.is_ge))
+        if d == 0:
+            V(ts(n, cnt, 1.0, A.is_ge, nlc, A.mult))
+        else:
+            V(tt(n, st, nl, A.mult))
+        zp, tot = pb(h, 1, 2), pb(h, 3)
+        P(group(half(zp, 0), [(PI4, zz), (I8, bb), (NI4, st), (T248, n)]) + group(half(zp, 1), [(PI4, zz), (NI4, st), (T256, n)])
+          + [mm(tot, ROLL if d else BLK, n)])
+        Z, yy, out, real = T_("Z", h, h16, W2), YY[h], pb(h, 4, 1, 1), T_("real", h, f32, HW)
+        V(tt(Z, zp, pay, A.add))
+        V(ts(real, tot, mneg, A.is_lt))
+        for c in range(4):
+            ss = range(4 * c, 4 * c + 4)
+            V([ts(sub(yy, s * W2, (s + 1) * W2), Z, 256.0 * (s - 8), A.max, 256.0 * (s - 7), A.min) for s in ss])
+            P(([mm(out, IC, ONES, True, False)] if c == 0 else []) +
+              [mm(out, sel(M, s, d), half(sub(yy, s * W2, (s + 1) * W2), j), False, s == 15 and j == 1) for s in ss for j, M in ((0, SEL256), (1, SELh))])
+        same = {"j1": "ta", "X": "ta", "sc": "ta", "i1": "ta", "j2": "tb", "xt": "tb", "i2": "tb", "mask": "tc", "r": "tc"}
+        f = lambda nm: T_(same.get(nm, nm), h, f32, HW)
+        real, j1, j2, X, xt, mask, sc, y2, i2 = [f(x) for x in ("real", "j1", "j2", "X", "xt", "mask", "sc", "y2", "i2")]
+        k2, i1, Lp, p1 = f("k2"), pb(h, 1), pb(h, 2), pb(h, 4)
+        ix = T_("ix", h, u16, HW)
+        V(ts(j1, out, 1.0 / 65792, A.mult, M23, A.add)); V(ts(j2, j1, M23 + 1.0, A.subtract, -65792.0, A.mult)); V(tt(X, out, j2, A.add))
+        V(tr(xt, X)); V(ts(mask, xt, 33793.0, A.is_le)); V(scan(sc, mask, xt, 33792.5, A.mult, A.max)); V(tr(k2, sc))
+        V(ts(y2, k2, M34, A.add, M34 + 65536.0, A.subtract))
+        if VIAPE:
+            P([mm(i1, IF, half(EM, h), True, False), mm(i1, IS, y2, False, True)])
+            V(ts(ix, i1, 16.0 * E - 1.0, A.min))
+        else:
+            V(ts(i1, y2, E / 2048.0, A.mult, cap, A.min)); V(tt(i2, i1, half(EM, h), A.add)); V(cp(ix, i2))
+        ad = f("ad")
+        S(act(ad, real, F.Identity, 65504.0, 27648.0 - 65504.0))
+        S(act(BG[h], ind(WIN[d], ix), F.Copy))
+        bx = pb(h, 3, 1, 1)
+        Lm = f("Lm")
+        P(group(Lp, [(IF, CT), (IF, k2), (NF, y2)]))
+        if d == 0:
+            V(ts(oP, Lp, -1184.0, A.add))
+        V(tt(Lm, Lp, real, A.mult))
+        P(group(bx, [(sel(EXT, k), sub(BG[h], k, WIDE, 16)) for k in range(16)]))
+        if d == 0:
+            V(ts(obb, y2, 1.0 / 2048, A.mult, m16, A.add))
+        p2, p3 = T_("p2", h, i32, HW), T_("p3", h, i32, HW)
+        V(tt(p1, bx, Lm, A.mult)); V(tt(p2, p1, ad, A.add))
+        V(ts(p3, p2, 5, A.arith_shift_right, NW - 1, A.bitwise_and)); V(cp(oL, p3))
+        return n
+
+    def split(h, nm, src):
+        pay = T_("pay" + nm, h, i32, W2)
+        V([ts(half(pay, 0), src, 8, A.arith_shift_right), ts(half(pay, 1), src, 255, A.bitwise_and)])
+        return pay
+
+    def hot(d, names):
+        hb, lh = T_("bhb", 0, b16, E), T_("blh", 0, h16, E)
+        at = 0
+        for x in names:
+            V([ts(sub(hb, at, at + wid(x)), x, 1.0 / 128, A.mult, 128.50390625, A.add), ts(sub(lh, at, at + wid(x)), x, 0.0, A.add)])
+            at += wid(x)
+        ins = []
+        for k in range(2):
+            for o, a, b in ((lambda c, n: bank(6, c + k * n, n), 0, 128), (lambda c, n: part(bank(6, c + 2 * n, n), 64 * k, 64 * k + 64), 128, E)):
+                ins += [mm(o(0, 128), sub(hb, a, b), ek(k))]
+                ins += group(o(384, 8), [(sub(lh, a, b), sub(E8h, 8 * k, 8 * k + 8)), (sub(hb, a, b), sub(E8n, 8 * k, 8 * k + 8))])
+        P(ins)
+        S(act(sub(LOC, 24 * d, 24 * d + 24), bank(6, 384, 24), F.Identity, 16512.0))
+        V(tt(sub(A0, 384 * d, 384 * d + 384), bank(6, 0, 384), HP, A.is_equal))
+        for c in range(3):
+            V([ts(sub(HOT, 128 * j, 128 * j + 128), IO, sub(LOC, j, j + 1), A.is_equal) for j in range(24 * d + 8 * c, 24 * d + 8 * c + 8)])
+
+    def reduce(d, h, src, out):
+        if d in RED:
+            for c in range(0, 16, PCUT):
+                P([mm(bank(RB[d], 0, HW), RF if d == 2 else IF, sub(src, k, WIDE, 16), k == 0, k == 15) for k in range(c, c + PCUT)])
+            S(act(out, bank(RB[d], 0, HW), F.Copy))
+            return
+        b = sub(SCB, d * SW, (d + 1) * SW + 8)
+        for c2 in range(2):
+            V([scan(sub(b, 136 * c + 8, 136 * c + 136), sub(src, 256 * c, 256 * c + 256, 2), sub(src, 256 * c + 1, 256 * c + 256, 2),
+                    0.0, A.add, A.add) for c in range(NC // 2 * c2, NC // 2 * (c2 + 1))])
+        V(tt(out, sub(b, 15, SW + 8, 8), sub(b, 7, SW, 8), A.subtract))
+
+    def fetch(out, win, lst, times=None, onv=False):
+        n = HW // CUT
+        for c in range(CUT):
+            o, x = sub(out, 16 * n * c, 16 * n * (c + 1)), ind(win, sub(lst, n * c, n * (c + 1)))
+            if onv:
+                V(cp(o, x))
+            elif times is None:
+                S(act(o, x, F.Copy))
+            else:
+                V(tt(o, x, sub(times, 16 * n * c, 16 * n * (c + 1)), A.mult))
+
+    def finish(t, D, Dn):
+        for h in range(NP):
+            yo, c0, bk = f32(HW), t * E + h * HW, bank(7, 0, HW)
+            three = [D[0][h], Dn[0][h], Dn[1][h]]
+            if len(RED) == 3:
+                P(group(bk, [(IF, x) for x in three]))
+                V(tt(yo, bk, sub(xv, c0, c0 + HW), A.mult))
+            else:
+                s1, s2 = T_("s1", h, f32, DW), T_("s2", h, f32, HW)
+                a, b = [three[d] for d in range(3) if d not in RED], [three[d] for d in RED]
+                if len(a) == 2:
+                    V(tt(s1, a[0], a[1], A.add)); V(tt(s2, ind(s1, sub(YL, 0, NC)), b[0], A.add))
+                    V(tt(yo, s2, sub(xv, c0, c0 + HW), A.mult))
+                else:
+                    V(tt(s2, ind(a[0], sub(YL, 0, NC)), b[0], A.add)); V(tt(bk, s2, b[1], A.add))
+                    V(tt(yo, bk, sub(xv, c0, c0 + HW), A.mult))
+            dma("Y", [(hbm("y", 0, 128, c0, c0 + HW), yo)], 2500, "outy")
+
+    def update(t, WG):
+        for d in range(3):
+            e = E0R if d == 2 else ek(0)
+            bk = bank(4 + d, 0, 384)
+            P([mm(sub(bk, 0, 128), sub(WG[d], 0, 128), e), mm(sub(bk, 128, 256), sub(WG[d], 0, 128), e),
+               mm(part(sub(bk, 256, 384), 0, 64), sub(WG[d], 128, E), e), mm(part(sub(bk, 256, 384), 64, 128), sub(WG[d], 128, E), e)])
+            V(tt(sub(AW, 384 * d, 384 * d + 384), bk, sub(A0, 384 * d, 384 * d + 384), A.mult))
+        ins = []
+        for g in range(8):
+            ins += group(bank(4, 16 * g, 16), [(sub(HOT, 128 * (8 * c + g), 128 * (8 * c + g) + 128), sub(AW, 128 * c + 16 * g, 128 * c + 16 * g + 16))
+                                               for c in range(9)])
+        P(ins)
+        m1, m2 = T_("m1", 0, b16, 128), T_("m2", 0, b16, 128)
+        V(ts(m1, bank(4, 0, 128), -0.5, A.max, 1.0, A.min))
+        P(mm(bank(5, 0, 128), m1, I1))
+        V(ts(m2, bank(5, 0, 128), 1.0, A.add))
+        for c in range(4):
+            bk = bank((6, 4, 5, 6)[c], 0, 512)
+            P([mm(sub(bk, 128 * j, 128 * j + 128), ek(4 * c + j), m2) for j in range(4)])
+            V(tt(sub(wU, 512 * c, 512 * c + 512), bk, sub(w, 512 * c, 512 * c + 512), A.mult))
+        for c in range(2):
+            V(ts(sub(w, 1024 * c, min(NW - 1, 1024 * c + 1024)), sub(wU, 1024 * c, min(NW - 1, 1024 * c + 1024)), 0.25, A.max, 4.0, A.min))
+        products(t + 1)
+
+    products(0)
+    windows(0, 0); windows(0, 1)
+    for t in range(EP):
+        last = t == EP - 1
+        PP = PT[t % 2]
+        dw = [HW if d in RED else DW for d in range(3)]
+        D = [[T_("d1%d" % (t % 2), h, f32, dw[0]) if d == 0 else f32(dw[d]) for h in range(NP)] for d in range(3)]
+        Dn = [[f32(dw[d]) for h in range(NP)] for d in (1, 2)]
+        names = [sub(bn, t * E, (t + 1) * E), T_("nm", 1, i32, E)]
+        WG = [b16(E), b16(E), b16(E)]
+        votes, vall, n3all = b16(E), b16(E), u16(E)
+        m12, m23 = [], []
+        for h in range(NP):
+            UP[0] = LEAD * (NP - 1 - h)
+            lst = half(sub(L1, t * E, (t + 1) * E), h)
+            ou, ob, nu, nb = u16(3 * HW), b16(HW), u16(3 * HW), T_("bb", h, b16, HW)
+            pay = split(h, "1", half(names[0], h))
+            cnt = strong(t, 0, h, lst)
+            children(t, 0, h, cnt, ob, pay, bb1, nl1, zz1, half(ou, 0), half(ou, 1), half(ou, 2))
+            send([(ou, [(1, nu)])])
+            n2, nr, b2 = u16(W2), u16(W2), b16(HW)
+            send([(ob, [(2, b2)])])
+            send([(sub(ou, 0, W2), [(2, n2)])])
+            dma("Y", [(part(nr, 16, 128), part(n2, 0, 112)), (part(nr, 0, 16), part(n2, 112, 128))], 2200)
+            m12.append((nu, nb, nr, b2))
+        if not last:
+            windows(t + 1, 0)
+            hot(0, [sub(L1, t * E, (t + 1) * E)])
+        keep = []
+        for h in range(NP):
+            UP[0] = LEAD * (NP - 1 - h)
+            nu, nb = m12[h][:2]
+            nl, zz, st = T_("nl", h, b16, HW), T_("zz", h, b16, HW), b16(HW)
+            V(cp(half(names[1], h), half(nu, 0)))
+            pay = split(h, "2", half(names[1], h))
+            V(ts(nb, half(nu, 2), 0.0, A.add))
+            V([ts(nl, half(nb, 0), 25.0, A.max, 31.0, A.subtract), ts(zz, half(nb, 0), 31.0, A.is_ge, 0.5, A.add)])
+            cnt = strong(t, 1, h, half(nu, 0))
+            o3, n3, nc = u16(HW), half(n3all, h), b16(HW)
+            keep.append(children(t, 1, h, cnt, st, pay, half(nb, 0), nl, zz, o3, None, None))
+            send([(st, [(1, nc)])])
+            send([(o3, [(1, n3)])])
+            m23.append((n3, nc))
+        if not last:
+            windows(t + 1, 1)
+            hot(1, [half(x[0], 0) for x in m12])
+        en, ef, ko, kn = T_("en", 0, b16, E), T_("ef", 0, f32, E), u16(E), u16(E)
+        P([mm(half(bank(5, 0, E), h), TRI, keep[h]) for h in range(NP)])
+        S(act(en, bank(5, 0, E), F.Copy))
+        for c in range(4):
+            ss = range(4 * c, 4 * c + 4)
+            if t in THV:
+                V([ts(sub(TH, s * E, (s + 1) * E), en, -float(s), A.is_ge, 0.5, A.subtract) for s in ss])
+            else:
+                S([act(sub(TH, s * E, (s + 1) * E), en, F.Sign, s + 0.5) for s in ss])
+            P([mm(bank(5, E, E), sel(SELb if t in THV else SELq, s, 1), sub(TH, s * E, (s + 1) * E), s == 0, s == 15) for s in ss])
+        V(tt(ef, bank(5, E, E), E16, A.add)); V(cp(ko, ef))
+        send([(ko, [(1, kn)])])
+        for h in range(NP):
+            UP[0] = LEAD * (NP - 1 - h)
+            n3, nc = m23[h]
+            st, vo = T_("st3", h, b16, HW), half(vall, h)
+            cnt = strong(t, 2, h, n3)
+            V(ts(st, cnt, 1.0, A.is_ge))
+            vt = pb(h, 3, 1, 1)
+            P(group(vt, [(BLK, m12[h][3]), (BLK, nc), (UNROLL, st)]))
+            if last:
+                V(cp(vo, vt))
+            else:
+                vd = lambda j: sub(VDn, 2 * E * j + t * E + h * HW, 2 * E * j + t * E + (h + 1) * HW)
+                po, pd = pb(h, 1), pb(h, 2)
+                V(tt(po, vt, vd(0), A.is_ge)); V(cp(vo, vt)); V(tt(pd, po, vd(1), A.subtract)); V(tt(half(WG[2], h), pd, vd(2), A.mult))
+                send([(half(WG[2], h), [(2, half(WG[0], h))]), (half(WG[2], h), [(3, half(WG[1], h))])])
+        UP[0] = 0.0
+        if not last:
+            hot(2, [n3all])
+        send([(vall, [(2, votes)])])
+        dma("G", [(hbm("cv", 0, 8, t * E, (t + 1) * E), part(votes, 0, 128, 16))], 2500, "outg")
+        for h in range(NP):
+            fetch(tv[0][h], PP, half(sub(L1, t * E, (t + 1) * E), h), None, (t, 0, h) in ONV)
+            reduce(0, h, tv[0][h], D[0][h])
+        if t:
+            finish(*todo)
+        for h in range(NP):
+            nu = m12[h][0]
+            fetch(av[h], ft, half(nu, 1))
+            fetch(tv[1][h], PP, half(nu, 0), av[h])
+            reduce(1, h, tv[1][h], D[1][h])
+            send([(D[1][h], [(3, Dn[0][h])])])
+        for h in range(NP):
+            nr = m12[h][2]
+            fetch(av[h], fR, half(nr, 1))
+            fetch(sub(v2[h], 0, WIDE), fR, half(nr, 0), av[h])
+            fetch(tv[0][h], PP, m23[h][0], None, (t, 2, h) in ONV)
+            fetch(tv[1][h], v2[h], half(kn, h), tv[0][h])
+            reduce(2, h, tv[1][h], D[2][h])
+            send([(D[2][h], [(2, Dn[1][h])])])
+        todo = (t, D, Dn)
+        if not last:
+            update(t, WG)
+    finish(*todo)
+
+
+def depend():
+    seen = {}
+    for i, o in enumerate(OPS):
+        deps = set()
+        for vs, wr in ((o["R"], False), (o["W"], True)):
+            for v in vs:
+                if v[0] not in ARENA and v[0][:2] != "ps":
+                    continue
+                ps = v[0][:2] == "ps"
+                a, b = (0, 512) if ps else (v[4], v[5])
+                for (j, a2, b2, w2) in seen.get(v[0], []):
+                    if j != i and a < b2 and a2 < b and (wr or w2 or (ps and OPS[j]["q"] != o["q"])):
+                        deps.add(j)
+        for vs, wr in ((o["R"], False), (o["W"], True)):
+            for v in vs:
+                ps = v[0][:2] == "ps"
+                a, b = (0, 512) if ps else (v[4], v[5])
+                l = seen.setdefault(v[0], [])
+                if wr and v[6] == 1 and (v[1], v[2], v[3]) == (0, 128, 1):
+                    l[:] = [x for x in l if x[0] == i or not (a <= x[1] and x[2] <= b)]
+                l.append((i, a, b, wr))
+        o["deps"] = sorted(deps)
+
+
+def schedule(slack=SLACK, same=60.0, other=110.0):
+    n = len(OPS)
+    kids = [[] for o in OPS]
+    for i, o in enumerate(OPS):
+        for j in o["deps"]:
+            kids[j].append(i)
+    pr = [0.0] * n
+    for i in range(n - 1, -1, -1):
+        pr[i] = OPS[i]["ns"] + OPS[i]["lat"] + max([pr[k] + other for k in kids[i]] + [0.0])
+    for i in range(n - 1, -1, -1):
+        pr[i] = max([pr[i] + OPS[i]["up"]] + [pr[k] + 1.0 for k in kids[i]])
+    best = top = None
+    rng = np.random.default_rng(SEED)
+    for turn in range(TURNS):
+        order = listing(pr, kids, slack, same, other)
+        at, span = replay(order, same, other)
+        if best is None or span < best[1] + HEAT * (1.0 - turn / TURNS):
+            if best is None or span < top[1]:
+                top = (order, span, at)
+            best = (order, span, at, list(pr))
+        pr = list(best[3])
+        a = int(rng.integers(0, n))
+        b = a + int(rng.integers(1, 40))
+        c = float(rng.normal()) * MIX
+        q = "VSP*"[int(rng.integers(0, 4))]
+        for i in range(n - 1, -1, -1):
+            move = c if a <= i < b and q in (OPS[i]["q"], "*") else 0.0
+            pr[i] = max([pr[i] + move] + [pr[k] + 1.0 for k in kids[i]])
+    best = top
+    for i in range(n):
+        OPS[i]["at"] = best[2][i]
+    return best[0], best[1]
+
+
+def listing(pr, kids, slack, same, other):
+    n = len(OPS)
+    fin, left = [None] * n, [len(o["deps"]) for o in OPS]
+    free, order = {q: 0.0 for q in "VSPGY"}, {q: [] for q in "VSPGY"}
+    pool = set(i for i in range(n) if left[i] == 0)
+    for step in range(n):
+        est, front = {}, sorted(pool)
+        for i in front:
+            o = OPS[i]
+            est[i] = max([o["late"], free[o["q"]]] + [fin[j] + (same if OPS[j]["q"] == o["q"] else other) for j in o["deps"]])
+        end = min(est.values()) + SIGHT
+        while front:
+            more = []
+            for i in front:
+                if est[i] + OPS[i]["ns"] + OPS[i]["lat"] < end:
+                    for k in kids[i]:
+                        if k not in est and all(fin[j] is not None or j in est for j in OPS[k]["deps"]):
+                            o = OPS[k]
+                            est[k] = max([o["late"], free[o["q"]]] + [(fin[j] if fin[j] is not None else est[j] + OPS[j]["ns"] + OPS[j]["lat"])
+                                                                      + (same if OPS[j]["q"] == o["q"] else other) for j in o["deps"]])
+                            more.append(k)
+            front = more
+        best = None
+        for c in pool:
+            q, e = OPS[c]["q"], est[c] + OPS[c]["ns"]
+            held = any(pr[i] > pr[c] + GAP and OPS[i]["q"] == q and est[i] + slack < e for i in est)
+            key = (held, est[c] // GRAIN, -pr[c], c)
+            if best is None or key < best:
+                best = key
+        c = best[3]
+        q = OPS[c]["q"]
+        pool.remove(c)
+        order[q].append(c)
+        free[q] = est[c] + OPS[c]["ns"]
+        fin[c] = free[q] + OPS[c]["lat"]
+        for k in kids[c]:
+            left[k] -= 1
+            if left[k] == 0:
+                pool.add(k)
+    return order
+
+
+def replay(order, same, other):
+    fin, at, free, pos = {}, [0.0] * len(OPS), {q: 0.0 for q in order}, {q: 0 for q in order}
+    go = True
+    while go:
+        go = False
+        for q in order:
+            while pos[q] < len(order[q]):
+                i = order[q][pos[q]]
+                o = OPS[i]
+                if any(j not in fin for j in o["deps"]):
+                    break
+                at[i] = max([free[q]] + [fin[j] + (same if OPS[j]["q"] == q else other) for j in o["deps"]])
+                free[q] = at[i] + o["ns"]
+                fin[i] = free[q] + o["lat"]
+                pos[q] += 1
+                go = True
+    return at, (max(fin.values()) if len(fin) == len(OPS) else 1e18)
+
+
+plan()
+depend()
+ORDER, SPAN = schedule()
+SCRATCH = {a: ("sbuf", [128, TOP[a]], ARENA[a]) for a in ARENA}
+for _b in range(8):
+    SCRATCH["ps%d" % _b] = ("psum", [128, 512], "float32")
+SEMAPHORES = list(SEMS)
+
+
+def rank_program(g, core, T, topo):
+    rank = T.rank_of(core)
+    if rank is None:
+        return
+    cores = list(T.cores)
+    n = len(cores)
+    lanes = [e for e in range(16) if all(e in topo.engines(a, b) for a in cores for b in cores if a != b)]
+    eng = {"V": g.vector, "S": g.scalar, "P": g.tensor, "G": g, "Y": g.sync}
+    mark, total = {}, {}
+    for q in ORDER:
+        for i in ORDER[q]:
+            o = OPS[i]
+            if o["kind"] == "c":
+                s, k = "c" + q, len(o["ins"])
+            elif o["kind"] == "d":
+                s, k = o["sem"], 16 * len(o["ins"])
+            else:
+                each = len(lanes) // len(o["x"])
+                s, k = o["sem"], sum(each * len(d) for src, d in o["x"])
+                total["sent"] = total.get("sent", 0) + each * len(o["x"])
+            total[s] = total.get(s, 0) + k
+            mark[i] = (s, total[s])
+    waited = {}
+    for q in ORDER:
+        e, have = eng[q], {}
+        for i in ORDER[q]:
+            o = OPS[i]
+            need = {}
+            for j in o["deps"]:
+                s, k = mark[j]
+                if not (q == "P" and s == "cP"):
+                    need[s] = max(need.get(s, 0), k)
+            for s in need:
+                if need[s] > have.get(s, 0):
+                    e.wait_ge(T.sem[s], need[s])
+                    have[s] = need[s]
+                    waited[s] = max(waited.get(s, 0), need[s])
+            if o["kind"] == "r":
+                each = len(lanes) // len(o["x"])
+                trs = []
+                for j, (src, dsts) in enumerate(o["x"]):
+                    ids = [topo.addr(cores[(rank + k) % n], core) for k, l in dsts]
+                    trs.append(RemoteDMATransfer(dst_ids=[DstId(rid=a, pnc=b) for a, b in ids],
+                                                 dma_engine_mask=sum(1 << x for x in lanes[j * each:(j + 1) * each]),
+                                                 remote_sem=T.sem[o["sem"]], srcs=[ap(T, src)], dsts=[ap(T, l) for k, l in dsts]))
+                g.remote_dma_fused(trs, local_sem=T.sem["sent"])
+                continue
+            for name, args, kw, r, w_, ns in o["ins"]:
+                x = [ap(T, v) for v in args]
+                kk = {k: ap(T, kw[k]) for k in kw}
+                done = call(e, name, x, kk)
+                done.then_inc(T.sem[mark[i][0]], 16 if o["kind"] == "d" else 1)
+    for s in total:
+        if total[s] > waited.get(s, 0):
+            g.wait_ge(T.sem[s], total[s])
+
+
+def call(e, name, x, kk):
+    if name == "tensor_tensor":
+        return e.tensor_tensor(*x)
+    if name == "tensor_scalar":
+        return e.tensor_scalar(*x)
+    if name == "tensor_copy":
+        return e.tensor_copy(*x)
+    if name == "transpose":
+        return e.transpose(*x)
+    if name == "tensor_tensor_scan":
+        return e.tensor_tensor_scan(*x)
+    if name == "memset":
+        return e.memset(*x)
+    if name == "activation":
+        return e.activation(*x, **kk)
+    if name == "matmul":
+        return e.matmul(*x)
+    if name == "iota":
+        return e.iota(*x, **kk)
+    if name == "affine_select":
+        return e.affine_select(*x)
+    return e.dma_start(*x)

@@ -163,8 +163,8 @@ def dma(q, pairs, lat, sem=None):
 def send(trs):
     sem = "r%d" % len(SEMS)
     SEMS.append(sem)
-    emit("G", [("send", (), {}, [s for s, d in trs], [l for s, d in trs for k, l in d], 600)], "r", sem, trs,
-         1500 + 800 * len(trs) * max(len(d) for s, d in trs))
+    emit("G", [("send", (), {}, [s for s, d in trs], [l for s, d in trs for k, l in d], 1300)], "r", sem, trs,
+         1500 + 500 * len(trs))
 
 
 def plan():
@@ -218,7 +218,7 @@ def plan():
     ONES = h16(HW); V(fill(ONES, 547.0))
     bb1, nl1, zz1, E16 = b16(HW), b16(HW), b16(HW), f32(E)
     V(ts(bb1, sub(EI, 0, HW), 0.0, A.mult, mcol, A.add)); V(ts(bb1, bb1, 16.0, A.add))
-    V(ts(nl1, bb1, 25.0, A.max, 31.0, A.subtract)); V(ts(zz1, bb1, 30.0, A.max, 29.5, A.subtract))
+    V(ts(nl1, bb1, 25.0, A.max, 31.0, A.subtract)); V(ts(zz1, nl1, -1.0, A.mult, -0.5, A.add)); V(ts(zz1, zz1, 0.5, A.max))
     V([ts(half(E16, h), sub(EI, 0, HW), 16.0, A.mult, 8.0, A.add) for h in range(NP)])
     SELq = b16(160)
     S(act(SELq, SELb, F.Copy, None, 0.5))
@@ -237,9 +237,8 @@ def plan():
     for t in range(EP):
         V([ts(hi_, sub(bn, t * E, (t + 1) * E), 5, A.arith_shift_right), ts(lo_, sub(bn, t * E, (t + 1) * E), 31, A.bitwise_and)])
         V([ts(sub(HL, 2 * t * E, (2 * t + 1) * E), hi_, 1.0, A.add), cp(sub(HL, (2 * t + 1) * E, (2 * t + 2) * E), lo_)])
-        if t != 1:
-            a = 0 if t == 0 else 2 * E
-            send([(sub(HL, a, (2 * t + 2) * E), [(1, sub(HLn, a, (2 * t + 2) * E))])])
+        if t == 0:
+            send([(sub(HL, 0, 2 * E), [(1, sub(HLn, 0, 2 * E))])])
     WIN = [b16(16 * E), b16(16 * E)]
     for j in range(2):
         dma("Y", [(sub(WIN[j], 0, NW), hbm("ft", 0, 128, 0, NW)), (sub(WIN[j], NW, 16 * E), hbm("ft", 0, 128, 0, 16 * E - NW))], 5000)
@@ -253,15 +252,15 @@ def plan():
     if len(RED) < 3:
         SCB = f32(2 * SW + 8)
         V(fill(sub(SCB, 7, 2 * SW + 8, 136), 0.0))
-    alb, REP, rp, VD, VDn = b16(4 * E), b16(128), i32(128), b16(6 * E), b16(6 * E)
+    alb, REP, rp, VD, VDn = b16(4 * E), b16(128), i32(128), b16(4 * E), b16(6 * E)
     emit("G", iota(part(rp, 0, 8), [[1, 128]], 0, -16))
     V(ts(part(rp, 0, 8), part(rp, 0, 8), 4, A.arith_shift_right)); V(ts(part(REP, 0, 8), part(rp, 0, 8), 0.0, A.is_equal))
     V(cp(part(alb, 0, 8), part(al, 0, 8)))
     P(mm(bank(4, 0, 2 * E), part(REP, 0, 8), part(sub(alb, 0, 2 * E), 0, 8)))
     P(mm(bank(5, 0, 2 * E), part(REP, 0, 8), part(sub(alb, 2 * E, 4 * E), 0, 8)))
     S(act(sub(VD, 0, 2 * E), bank(4, 0, 2 * E), F.Copy)); S(act(sub(VD, 2 * E, 4 * E), bank(5, 0, 2 * E), F.Copy))
-    V(ts(sub(VD, 4 * E, 6 * E), sub(VD, 2 * E, 4 * E), -4095.0, A.mult, -1.0, A.add))
-    send([(VD, [(2, VDn)])])
+    send([(VD, [(2, sub(VDn, 0, 4 * E))]), (sub(HL, 2 * E, 6 * E), [(1, sub(HLn, 2 * E, 6 * E))])])
+    S(act(sub(VDn, 4 * E, 6 * E), sub(VDn, 2 * E, 4 * E), F.Identity, -1.0, -4095.0))
     EK, hc, E0R, HP, IO = b16(NW), f32(1), b16(128), b16(384), b16(128)
     emit("G", iota(EK, [[0, NW]], 1, 0), late=7000.0)
     emit("G", pick(EK, EK, [[-1, 16], [-16, 8], [0, 16]], 0, 1))
@@ -318,8 +317,8 @@ def plan():
             V(ts(n, cnt, 1.0, A.is_ge, nlc, A.mult))
         else:
             V(tt(n, st, nl, A.mult))
-        zp, tot = pb(h, 1, 2), pb(h, 3)
-        P(group(half(zp, 0), [(PI4, zz), (I8, bb), (NI4, st), (T248, n)]) + group(half(zp, 1), [(PI4, zz), (NI4, st), (T256, n)])
+        zp, tot, big = pb(h, 1, 2), pb(h, 3), (NI4, st) if d else (PI4, n)
+        P(group(half(zp, 0), [(PI4, zz), (I8, bb), big, (T248, n)]) + group(half(zp, 1), [(PI4, zz), big, (T256, n)])
           + [mm(tot, ROLL if d else BLK, n)])
         Z, yy, out, real = T_("Z", h, h16, W2), YY[h], pb(h, 4, 1, 1), T_("real", h, f32, HW)
         V(tt(Z, zp, pay, A.add))
@@ -451,26 +450,23 @@ def plan():
     for t in range(EP):
         last = t == EP - 1
         PP = PT[t % 2]
-        dw = [HW if d in RED else DW for d in range(3)]
-        D = [[T_("d1%d" % (t % 2), h, f32, dw[0]) if d == 0 else f32(dw[d]) for h in range(NP)] for d in range(3)]
-        Dn = [[f32(dw[d]) for h in range(NP)] for d in (1, 2)]
         names = [sub(bn, t * E, (t + 1) * E), T_("nm", 1, i32, E)]
         WG = [b16(E), b16(E), b16(E)]
-        votes, vall, n3all = b16(E), b16(E), u16(E)
+        votes, vall, n3all = f32(E), f32(E), u16(E)
+        on, on2, onr = u16(5 * E), u16(5 * E), T_("onr", t % 2, u16, 4 * E)
+        Da, Dna = [f32(E), f32(E)], [f32(E), f32(E)]
+        D = [[T_("d1%d" % (t % 2), h, f32, HW) for h in range(NP)]] + [[half(x, h) for h in range(NP)] for x in Da]
+        Dn = [[half(x, h) for h in range(NP)] for x in Dna]
         m12, m23 = [], []
         for h in range(NP):
             UP[0] = LEAD * (NP - 1 - h)
             lst = half(sub(L1, t * E, (t + 1) * E), h)
-            ou, ob, nu, nb = u16(3 * HW), b16(HW), u16(3 * HW), T_("bb", h, b16, HW)
+            ou, nu, nb = T_("ou%d" % t, h, u16, 4 * HW), sub(on, 4 * HW * h, 4 * HW * (h + 1)), T_("bb", h, b16, W2)
             pay = split(h, "1", half(names[0], h))
             cnt = strong(t, 0, h, lst)
-            children(t, 0, h, cnt, ob, pay, bb1, nl1, zz1, half(ou, 0), half(ou, 1), half(ou, 2))
+            children(t, 0, h, cnt, half(ou, 3), pay, bb1, nl1, zz1, half(ou, 0), half(ou, 1), half(ou, 2))
             send([(ou, [(1, nu)])])
-            n2, nr, b2 = u16(W2), u16(W2), b16(HW)
-            send([(ob, [(2, b2)])])
-            send([(sub(ou, 0, W2), [(2, n2)])])
-            dma("Y", [(part(nr, 16, 128), part(n2, 0, 112)), (part(nr, 0, 16), part(n2, 112, 128))], 2200)
-            m12.append((nu, nb, nr, b2))
+            m12.append((nu, nb, sub(onr, 4 * HW * h, 4 * HW * (h + 1))))
         if not last:
             windows(t + 1, 0)
             hot(0, [sub(L1, t * E, (t + 1) * E)])
@@ -478,21 +474,22 @@ def plan():
         for h in range(NP):
             UP[0] = LEAD * (NP - 1 - h)
             nu, nb = m12[h][:2]
-            nl, zz, st = T_("nl", h, b16, HW), T_("zz", h, b16, HW), b16(HW)
+            nl, zz, st = T_("nl", h, b16, HW), T_("zz", h, b16, HW), T_("st2", h, b16, HW)
             V(cp(half(names[1], h), half(nu, 0)))
             pay = split(h, "2", half(names[1], h))
-            V(ts(nb, half(nu, 2), 0.0, A.add))
+            V(ts(nb, sub(nu, W2, 2 * W2), 0.0, A.add))
             V([ts(nl, half(nb, 0), 25.0, A.max, 31.0, A.subtract), ts(zz, half(nb, 0), 31.0, A.is_ge, 0.5, A.add)])
             cnt = strong(t, 1, h, half(nu, 0))
             o3, n3, nc = u16(HW), half(n3all, h), b16(HW)
             keep.append(children(t, 1, h, cnt, st, pay, half(nb, 0), nl, zz, o3, None, None))
-            send([(st, [(1, nc)])])
-            send([(o3, [(1, n3)])])
+            oc = b16(HW)
+            V(tt(oc, st, half(nb, 1), A.add))
+            send([(o3, [(1, n3)]), (oc, [(1, nc)])])
             m23.append((n3, nc))
         if not last:
             windows(t + 1, 1)
             hot(1, [half(x[0], 0) for x in m12])
-        en, ef, ko, kn = T_("en", 0, b16, E), T_("ef", 0, f32, E), u16(E), u16(E)
+        en, ef, ko, kn = T_("en", 0, b16, E), T_("ef", 0, f32, E), sub(on, 4 * E, 5 * E), sub(on2, 4 * E, 5 * E)
         P([mm(half(bank(5, 0, E), h), TRI, keep[h]) for h in range(NP)])
         S(act(en, bank(5, 0, E), F.Copy))
         for c in range(4):
@@ -503,7 +500,9 @@ def plan():
                 S([act(sub(TH, s * E, (s + 1) * E), en, F.Sign, s + 0.5) for s in ss])
             P([mm(bank(5, E, E), sel(SELb if t in THV else SELq, s, 1), sub(TH, s * E, (s + 1) * E), s == 0, s == 15) for s in ss])
         V(tt(ef, bank(5, E, E), E16, A.add)); V(cp(ko, ef))
-        send([(ko, [(1, kn)])])
+        send([(on, [(1, on2)])])
+        n2 = sub(on2, 0, 4 * E)
+        dma("Y", [(part(onr, 16, 128), part(n2, 0, 112)), (part(onr, 0, 16), part(n2, 112, 128))], 2400)
         for h in range(NP):
             UP[0] = LEAD * (NP - 1 - h)
             n3, nc = m23[h]
@@ -511,19 +510,17 @@ def plan():
             cnt = strong(t, 2, h, n3)
             V(ts(st, cnt, 1.0, A.is_ge))
             vt = pb(h, 3, 1, 1)
-            P(group(vt, [(BLK, m12[h][3]), (BLK, nc), (UNROLL, st)]))
+            P(group(vt, [(BLK, nc), (UNROLL, st)]))
             if last:
                 V(cp(vo, vt))
             else:
                 vd = lambda j: sub(VDn, 2 * E * j + t * E + h * HW, 2 * E * j + t * E + (h + 1) * HW)
                 po, pd = pb(h, 1), pb(h, 2)
                 V(tt(po, vt, vd(0), A.is_ge)); V(cp(vo, vt)); V(tt(pd, po, vd(1), A.subtract)); V(tt(half(WG[2], h), pd, vd(2), A.mult))
-                send([(half(WG[2], h), [(2, half(WG[0], h))]), (half(WG[2], h), [(3, half(WG[1], h))])])
         UP[0] = 0.0
         if not last:
+            send([(WG[2], [(2, WG[0])]), (WG[2], [(3, WG[1])])])
             hot(2, [n3all])
-        send([(vall, [(2, votes)])])
-        dma("G", [(hbm("cv", 0, 8, t * E, (t + 1) * E), part(votes, 0, 128, 16))], 2500, "outg")
         for h in range(NP):
             fetch(tv[0][h], PP, half(sub(L1, t * E, (t + 1) * E), h), None, (t, 0, h) in ONV)
             reduce(0, h, tv[0][h], D[0][h])
@@ -534,7 +531,8 @@ def plan():
             fetch(av[h], ft, half(nu, 1))
             fetch(tv[1][h], PP, half(nu, 0), av[h])
             reduce(1, h, tv[1][h], D[1][h])
-            send([(D[1][h], [(3, Dn[0][h])])])
+        if last:
+            send([(Da[0], [(3, Dna[0])])])
         for h in range(NP):
             nr = m12[h][2]
             fetch(av[h], fR, half(nr, 1))
@@ -542,7 +540,8 @@ def plan():
             fetch(tv[0][h], PP, m23[h][0], None, (t, 2, h) in ONV)
             fetch(tv[1][h], v2[h], half(kn, h), tv[0][h])
             reduce(2, h, tv[1][h], D[2][h])
-            send([(D[2][h], [(2, Dn[1][h])])])
+        send([(Da[1], [(2, Dna[1])]), (vall, [(2, votes)])] + ([] if last else [(Da[0], [(3, Dna[0])])]))
+        dma("Y", [(hbm("cv", 0, 8, t * E, (t + 1) * E), part(votes, 0, 128, 16))], 2500, "outy")
         todo = (t, D, Dn)
         if not last:
             update(t, WG)
@@ -677,6 +676,14 @@ for _b in range(8):
 SEMAPHORES = list(SEMS)
 
 
+def deal(lanes, n):
+    out = []
+    for j in range(n - 1):
+        out.append(lanes[:len(lanes) // 2])
+        lanes = lanes[len(lanes) // 2:]
+    return out + [lanes]
+
+
 def rank_program(g, core, T, topo):
     rank = T.rank_of(core)
     if rank is None:
@@ -694,9 +701,9 @@ def rank_program(g, core, T, topo):
             elif o["kind"] == "d":
                 s, k = o["sem"], 16 * len(o["ins"])
             else:
-                each = len(lanes) // len(o["x"])
-                s, k = o["sem"], sum(each * len(d) for src, d in o["x"])
-                total["sent"] = total.get("sent", 0) + each * len(o["x"])
+                cut = deal(lanes, len(o["x"]))
+                s, k = o["sem"], sum(len(c) * len(x[1]) for c, x in zip(cut, o["x"]))
+                total["sent"] = total.get("sent", 0) + sum(len(c) for c in cut)
             total[s] = total.get(s, 0) + k
             mark[i] = (s, total[s])
     waited = {}
@@ -715,12 +722,12 @@ def rank_program(g, core, T, topo):
                     have[s] = need[s]
                     waited[s] = max(waited.get(s, 0), need[s])
             if o["kind"] == "r":
-                each = len(lanes) // len(o["x"])
+                cut = deal(lanes, len(o["x"]))
                 trs = []
                 for j, (src, dsts) in enumerate(o["x"]):
                     ids = [topo.addr(cores[(rank + k) % n], core) for k, l in dsts]
                     trs.append(RemoteDMATransfer(dst_ids=[DstId(rid=a, pnc=b) for a, b in ids],
-                                                 dma_engine_mask=sum(1 << x for x in lanes[j * each:(j + 1) * each]),
+                                                 dma_engine_mask=sum(1 << x for x in cut[j]),
                                                  remote_sem=T.sem[o["sem"]], srcs=[ap(T, src)], dsts=[ap(T, l) for k, l in dsts]))
                 g.remote_dma_fused(trs, local_sem=T.sem["sent"])
                 continue

import numpy as np
from concourse.bass import DstId, RemoteDMATransfer
from concourse.mybir import AluOpType as A, ActivationFunctionType as F

NW, E, EP, HW = 2048, 192, 3, 64
NP, W2, WIDE, NC = E // HW, 2 * HW, 16 * HW, HW // 16
DW, SW = 17 * NC, 136 * NC
ARENA = {"af": "float32", "ab": "bfloat16", "ah": "float16", "ai": "int32", "au": "uint16"}
SIZE = {"af": 4, "ab": 2, "ah": 2, "ai": 4, "au": 2}
TOP = {k: 0 for k in ARENA}
OPS, SEMS = [], ["cV", "cS", "cP", "cG", "sent"]
CY, PC = 0.92, 0.47
RED = (0, 1, 2)
RB = (3, 7, 7)
SIGHT, GAP, GRAIN = 3000.0, 5000.0, 50.0
VIAPE = True
THV, ONV = (2,), ()
SLACK, TURNS, MIX, CUT, PCUT = 300.0, 1, 3000.0, 2, 4
HEAT, SEED, LEAD, UP = 300.0, 1, 1500.0, [0.0]


def alloc(a, n):
    c = TOP[a]
    TOP[a] = c + (n + 15) // 16 * 16
    return (a, 0, 128, 1, c, c + n, 1)


def sub(v, a, b, s=1):
    return v[:4] + (v[4] + a, v[4] + b, s)


def part(v, a, b, s=1):
    return (v[0], a, b, s) + v[4:]


def bank(b, a, n):
    return ("ps%d" % b, 0, 128, 1, a, a + n, 1)


def pb(h, u, n=1, second=0):
    return bank(2 * h + second if NP == 2 else h, u * HW, n * HW)


def hbm(name, r0, r1, c0, c1):
    return (name, r0, r1, 1, c0, c1, 1)


def wid(v):
    return (v[5] - v[4] + v[6] - 1) // v[6]


def isv(x):
    return isinstance(x, tuple)


def ap(T, v):
    if not isv(v):
        return v
    if v[0] == "ind":
        return ap(T, v[1]).indirect(ap(T, v[2]))
    return T[v[0]][v[1]:v[2]:v[3], v[4]:v[5]:v[6]]


def ind(win, off):
    return ("ind", win, off)


def views(xs):
    out = []
    for x in xs:
        if isv(x):
            out += [x[1], x[2]] if x[0] == "ind" else [x]
    return out


def narrow(vs):
    return all(SIZE.get(v[0], 4) == 2 for v in vs)


def vcost(out, ins, rate):
    if any(isv(x) and x[0] == "ind" for x in ins):
        return 55 + wid(out) * 1.56 * CY
    return 25 + max(64, wid(out) * rate) * CY


def tt(out, a, b, op):
    r = 1 if a[0][:2] == "ps" or b[0][:2] == "ps" else 2
    return ("tensor_tensor", (out, a, b, op), {}, views([a, b]), [out], vcost(out, [a], r))


def ts(out, a, s1, o1, s2=None, o2=None):
    args = (out, a, s1, s2, o1) + (() if o2 is None else (o2,))
    return ("tensor_scalar", args, {}, views([a, s1, s2]), [out], vcost(out, [a], 0.5 if narrow([out, a]) else 1))


def cp(out, a):
    return ("tensor_copy", (out, a), {}, views([a]), [out], vcost(out, [a], 0.5 if narrow([out, a]) else 1))


def tr(out, a):
    return ("transpose", (out, a), {}, [a], [out], vcost(out, [a], 0.5 if narrow([out, a]) else 1))


def scan(out, a, b, init, o0, o1):
    return ("tensor_tensor_scan", (out, a, b, init, o0, o1), {}, [a, b], [out], vcost(out, [a], 1))


def fill(out, c):
    return ("memset", (out, c), {}, [], [out], vcost(out, [], 0.5 if narrow([out]) else 1))


def act(out, a, f, bias=None, scale=None):
    kw = {} if bias is None else {"bias": bias}
    if scale is not None:
        kw["scale"] = scale
    return ("activation", (out, a, f), kw, views([a, bias, scale]), [out], vcost(out, [a], 1) + 15)


def mm(out, l, r, start=True, stop=True):
    c = max(min(64, wid(l)), wid(r)) * (4 if l[0] == "af" else 1) * PC
    return ("matmul", (out, l, r, start, stop), {}, [l, r], [out], c)


def iota(out, pat, base, cm):
    kw = {} if out[0] == "ai" else {"allow_small_or_imprecise_dtypes": True}
    return ("iota", (out, pat, base, cm), kw, [], [out], 150 + 2 * CY * wid(out))


def pick(out, a, pat, base, cm):
    return ("affine_select", (out, a, pat, A.is_equal, 0.0, base, cm), {}, [a], [out], 190 + 2 * CY * wid(out))


def emit(q, ins, kind="c", sem=None, extra=None, lat=0, late=0.0):
    ins = ins if isinstance(ins, list) else [ins]
    OPS.append({"q": q, "ins": ins, "kind": kind, "sem": sem, "x": extra, "lat": lat, "late": late, "up": UP[0],
                "R": [v for i in ins for v in i[3]], "W": [v for i in ins for v in i[4]], "ns": sum(i[5] for i in ins)})


def V(i):
    emit("V", i)


def S(i):
    emit("S", i)


def P(i):
    emit("P", i)


def group(out, pairs):
    return [mm(out, l, r, j == 0, j == len(pairs) - 1) for j, (l, r) in enumerate(pairs)]


def dma(q, pairs, lat, sem=None):
    if sem is None:
        sem = "d%d" % len(SEMS)
    if sem not in SEMS:
        SEMS.append(sem)
    emit(q, [("dma_start", (o, i), {}, [i], [o], 60 if q != "G" else 900) for o, i in pairs], "d", sem, None, lat)


def send(trs):
    sem = "r%d" % len(SEMS)
    SEMS.append(sem)
    emit("G", [("send", (), {}, [s for s, d in trs], [l for s, d in trs for k, l in d], 1300)], "r", sem, trs,
         1500 + 500 * len(trs))


def plan():
    f32 = lambda n: alloc("af", n)
    b16 = lambda n: alloc("ab", n)
    h16 = lambda n: alloc("ah", n)
    i32 = lambda n: alloc("ai", n)
    u16 = lambda n: alloc("au", n)
    half = lambda v, h: sub(v, h * HW, (h + 1) * HW)

    w, wU, ft, fR = b16(NW), b16(NW), b16(NW), b16(NW)
    bn, tau, xv, al = i32(EP * E), f32(3), b16(EP * E), i32(4 * E)
    dma("Y", [(w, hbm("wt", 0, 128, 0, NW))], 3200)
    dma("S", [(tau, hbm("tau", 0, 128, 0, 3))], 1800)
    dma("S", [(bn, hbm("bn", 0, 128, 0, EP * E))], 2400)
    dma("Y", [(ft, hbm("ft", 0, 128, 0, NW))], 4500)
    dma("Y", [(part(sub(al, 0, 2 * E), 0, 8), hbm("ask", 0, 8, 0, 2 * E)), (part(sub(al, 2 * E, 4 * E), 0, 8), hbm("lab", 0, 8, 0, 2 * E))], 3000)
    dma("Y", [(part(fR, 16, 128), hbm("ft", 0, 112, 0, NW)), (part(fR, 0, 16), hbm("ft", 112, 128, 0, NW))], 6000)
    dma("Y", [(xv, hbm("xv", 0, 128, 0, EP * E))], 6000)

    CP, PI, EI = i32(E), i32(1), i32(E)
    emit("G", iota(PI, [[1, 1]], 0, 1))
    emit("G", iota(EI, [[1, E]], 0, 0))
    emit("G", iota(CP, [[1, 128]], 0, -1) if False else iota(sub(CP, 0, 128), [[1, 128]], 0, -1))
    mi, gi, mcol, gcol = i32(1), i32(1), f32(1), f32(1)
    V(ts(mi, PI, 15, A.bitwise_and)); V(ts(gi, PI, 112, A.bitwise_and)); V(cp(mcol, mi)); V(cp(gcol, gi))
    t160, u160 = i32(160), i32(160)
    SELb, SELh, EXT, BW = b16(160), h16(160), b16(160), b16(160)
    V(ts(t160, sub(EI, 0, 160), gcol, A.subtract, 96.0, A.add))
    V(ts(u160, t160, 127, A.bitwise_and))
    V(ts(SELb, u160, 0.0, A.is_equal)); V(cp(SELh, SELb))
    sel = lambda M, s, roll=0: sub(M, 32 - s - 16 * roll, 160 - s - 16 * roll)
    x0, x1 = f32(1), f32(1)
    V(ts(x0, mcol, 0.0, A.is_equal, 32.0, A.mult)); V(ts(x1, mcol, 1.0, A.is_equal, x0, A.add))
    S(act(EXT, SELb, F.Identity, None, x1))
    t2, u2 = i32(160), i32(160)
    V(ts(t2, t160, 16.0, A.add)); V(ts(u2, t2, 112, A.bitwise_and)); V(ts(BW, u2, 0.0, A.is_equal))
    BLK, ROLL, UNROLL = sub(BW, 16, 144), sub(BW, 0, 128), sub(BW, 32, 160)
    cp128 = sub(CP, 0, 128)
    I1, I8, PI4, NI4, T256, T248, tri, IC, RF = b16(128), b16(128), b16(128), b16(128), b16(128), b16(128), b16(128), h16(128), f32(128)
    V(ts(tri, cp128, 0.0, A.is_gt)); V(tt(tri, tri, BLK, A.mult))
    V(ts(I1, cp128, 0.0, A.is_equal))
    S([act(M, x, F.Copy, None, c) for M, x, c in ((T256, tri, -256.0), (T248, tri, -248.0))])
    S([act(M, I1, F.Copy, None, c) for M, c in ((NI4, -4096.0), (PI4, 4096.0), (I8, 8.0))])
    V(ts(IC, I1, -58.5, A.mult))
    SEL256, TRI = h16(160), b16(128)
    V(ts(SEL256, SELb, 256.0, A.mult))
    V(tt(TRI, tri, I1, A.add))
    rt, ru = i32(128), i32(128)
    V(ts(rt, cp128, 144.0, A.add)); V(ts(ru, rt, 127, A.bitwise_and)); V(ts(RF, ru, 0.0, A.is_equal))
    ONES = h16(HW); V(fill(ONES, 547.0))
    bb1, nl1, zz1, E16 = b16(HW), b16(HW), b16(HW), f32(E)
    V(ts(bb1, sub(EI, 0, HW), 0.0, A.mult, mcol, A.add)); V(ts(bb1, bb1, 16.0, A.add))
    V(ts(nl1, bb1, 25.0, A.max, 31.0, A.subtract)); V(ts(zz1, nl1, -1.0, A.mult, -0.5, A.add)); V(ts(zz1, zz1, 0.5, A.max))
    V([ts(half(E16, h), sub(EI, 0, HW), 16.0, A.mult, 8.0, A.add) for h in range(NP)])
    SELq = b16(160)
    S(act(SELq, SELb, F.Copy, None, 0.5))
    nlc, m192, cap, mneg, m16, EM = f32(1), f32(1), f32(1), f32(1), f32(1), f32(E)
    V(cp(nlc, sub(nl1, 0, 1)))
    V(ts(m192, mcol, float(E), A.mult)); V(ts(cap, m192, -1.0, A.mult, 15.0 * E, A.add))
    V(ts(mneg, mcol, -1.0, A.mult)); V(ts(m16, mcol, 16.0, A.add)); V(ts(EM, EI, m192, A.add))
    YL, yl = u16(8), f32(8)
    V(ts(yl, sub(EI, 0, 8), 17.0, A.mult, mcol, A.add)); V(cp(YL, yl))
    a0, a1, a2, a3, nth = f32(3), i32(3), f32(3), f32(3), f32(3)
    V(ts(a0, tau, 512.0, A.mult)); V(cp(a1, a0)); V(cp(a2, a1)); V(tt(a3, a2, a0, A.is_lt)); V(tt(a2, a2, a3, A.add))
    V(ts(a3, a2, 128.0, A.is_equal, 96.0, A.mult)); V(tt(a2, a3, a2, A.subtract)); V(ts(nth, a2, 0.25, A.add, 1.0 / 512, A.mult))
    L1 = u16(EP * E)
    V(cp(sub(L1, 0, E), sub(bn, 0, E))); V(cp(sub(L1, E, EP * E), sub(bn, E, EP * E)))
    HL, HLn, hi_, lo_ = b16(2 * EP * E), b16(2 * EP * E), i32(E), i32(E)
    for t in range(EP):
        V([ts(hi_, sub(bn, t * E, (t + 1) * E), 5, A.arith_shift_right), ts(lo_, sub(bn, t * E, (t + 1) * E), 31, A.bitwise_and)])
        V([ts(sub(HL, 2 * t * E, (2 * t + 1) * E), hi_, 1.0, A.add), cp(sub(HL, (2 * t + 1) * E, (2 * t + 2) * E), lo_)])
        if t == 0:
            send([(sub(HL, 0, 2 * E), [(1, sub(HLn, 0, 2 * E))])])
    WIN = [b16(16 * E), b16(16 * E)]
    for j in range(2):
        dma("Y", [(sub(WIN[j], 0, NW), hbm("ft", 0, 128, 0, NW)), (sub(WIN[j], NW, 16 * E), hbm("ft", 0, 128, 0, 16 * E - NW))], 5000)
    IF = f32(128)
    S(act(IF, I1, F.Copy))
    NF, CT = f32(128), f32(HW)
    S(act(NF, I1, F.Copy, None, -1.0)); V(fill(CT, -63328.5))
    if VIAPE:
        IS = f32(128)
        S(act(IS, I1, F.Copy, None, E / 2048.0))
    if len(RED) < 3:
        SCB = f32(2 * SW + 8)
        V(fill(sub(SCB, 7, 2 * SW + 8, 136), 0.0))
    alb, REP, rp, VD, VDn = b16(4 * E), b16(128), i32(128), b16(4 * E), b16(6 * E)
    emit("G", iota(part(rp, 0, 8), [[1, 128]], 0, -16))
    V(ts(part(rp, 0, 8), part(rp, 0, 8), 4, A.arith_shift_right)); V(ts(part(REP, 0, 8), part(rp, 0, 8), 0.0, A.is_equal))
    V(cp(part(alb, 0, 8), part(al, 0, 8)))
    P(mm(bank(4, 0, 2 * E), part(REP, 0, 8), part(sub(alb, 0, 2 * E), 0, 8)))
    P(mm(bank(5, 0, 2 * E), part(REP, 0, 8), part(sub(alb, 2 * E, 4 * E), 0, 8)))
    S(act(sub(VD, 0, 2 * E), bank(4, 0, 2 * E), F.Copy)); S(act(sub(VD, 2 * E, 4 * E), bank(5, 0, 2 * E), F.Copy))
    send([(VD, [(2, sub(VDn, 0, 4 * E))]), (sub(HL, 2 * E, 6 * E), [(1, sub(HLn, 2 * E, 6 * E))])])
    S(act(sub(VDn, 4 * E, 6 * E), sub(VDn, 2 * E, 4 * E), F.Identity, -1.0, -4095.0))
    EK, hc, E0R, HP, IO = b16(NW), f32(1), b16(128), b16(384), b16(128)
    emit("G", iota(EK, [[0, NW]], 1, 0), late=7000.0)
    emit("G", pick(EK, EK, [[-1, 16], [-16, 8], [0, 16]], 0, 1))
    V(ts(hc, mcol, 0.0, A.is_equal)); V(ts(E0R, ROLL, hc, A.mult))
    E8h, E8n = h16(16), b16(16)
    V([cp(E8h, sub(EK, 0, 256, 16)), ts(E8n, sub(EK, 0, 256, 16), -128.0, A.mult)])
    emit("G", iota(HP, [[0, 24], [1, 16]], 129, 0), late=7000.0)
    emit("G", iota(IO, [[1, 128]], 0, 0), late=7000.0)
    ek = lambda k: sub(EK, 128 * k, 128 * k + 128)

    PT = [f32(NW), f32(NW)]
    SG = BG = [b16(WIDE) for h in range(NP)]
    YY = [h16(16 * W2) for h in range(NP)]
    tv = [[f32(WIDE) for h in range(NP)] for d in range(2)]
    v2 = [f32(WIDE + 16) for h in range(NP)]
    V([fill(sub(v2[h], WIDE, WIDE + 16), 0.0) for h in range(NP)])
    TH = b16(NP * WIDE)
    av = [sub(TH, h * WIDE, (h + 1) * WIDE) for h in range(NP)]
    HOT, A0, AW, LOC = b16(72 * 128), b16(1152), b16(1152), b16(72)
    tmp = {}

    def T_(name, h, mk, n):
        if (name, h) not in tmp:
            tmp[(name, h)] = mk(n)
        return tmp[(name, h)]

    M23, M34 = 1.5 * 2.0 ** 23, 1.5 * 2.0 ** 34

    def products(t):
        for c in range(4):
            s = lambda v: sub(v, 512 * c, 512 * c + 512)
            bk = bank((4, 5, 6, 4)[c], 0, 512)
            P(mm(bk, I1, s(w)))
            V(tt(s(PT[t % 2]), bk, s(ft), A.mult))

    def windows(t, j):
        for k in range(2):
            src = sub(HLn if j else HL, (2 * t + k) * E, (2 * t + k + 1) * E)
            if j:
                dma("Y", [(part(WIN[1], 16 + k, 128, 16), part(src, 0, 112)), (part(WIN[1], k, k + 1), part(src, 112, 128))], 2500)
            else:
                dma("Y", [(part(WIN[0], k, 128, 16), src)], 2500)

    def strong(t, d, h, lst):
        S(act(SG[h], ind(w if t == 0 else wU, lst), F.Sign, sub(nth, d, d + 1)))
        cnt = pb(h, 0)
        P(group(cnt, [(sel(SELb, k), sub(SG[h], k, WIDE, 16)) for k in range(16)]))
        return cnt

    def children(t, d, h, cnt, st, pay, bb, nl, zz, oL, oP, obb):
        n = T_("n%d" % d, h, b16, HW)
        V(ts(st, cnt, 1.0, A.is_ge))
        if d == 0:
            V(ts(n, cnt, 1.0, A.is_ge, nlc, A.mult))
        else:
            V(tt(n, st, nl, A.mult))
        zp, tot, big = pb(h, 1, 2), pb(h, 3), (NI4, st) if d else (PI4, n)
        P(group(half(zp, 0), [(PI4, zz), (I8, bb), big, (T248, n)]) + group(half(zp, 1), [(PI4, zz), big, (T256, n)])
          + [mm(tot, ROLL if d else BLK, n)])
        Z, yy, out, real = T_("Z", h, h16, W2), YY[h], pb(h, 4, 1, 1), T_("real", h, f32, HW)
        V(tt(Z, zp, pay, A.add))
        V(ts(real, tot, mneg, A.is_lt))
        for c in range(4):
            ss = range(4 * c, 4 * c + 4)
            V([ts(sub(yy, s * W2, (s + 1) * W2), Z, 256.0 * (s - 8), A.max, 256.0 * (s - 7), A.min) for s in ss])
            P(([mm(out, IC, ONES, True, False)] if c == 0 else []) +
              [mm(out, sel(M, s, d), half(sub(yy, s * W2, (s + 1) * W2), j), False, s == 15 and j == 1) for s in ss for j, M in ((0, SEL256), (1, SELh))])
        same = {"j1": "ta", "X": "ta", "sc": "ta", "i1": "ta", "j2": "tb", "xt": "tb", "i2": "tb", "mask": "tc", "r": "tc"}
        f = lambda nm: T_(same.get(nm, nm), h, f32, HW)
        real, j1, j2, X, xt, mask, sc, y2, i2 = [f(x) for x in ("real", "j1", "j2", "X", "xt", "mask", "sc", "y2", "i2")]
        k2, i1, Lp, p1 = f("k2"), pb(h, 1), pb(h, 2), pb(h, 4)
        ix = T_("ix", h, u16, HW)
        V(ts(j1, out, 1.0 / 65792, A.mult, M23, A.add)); V(ts(j2, j1, M23 + 1.0, A.subtract, -65792.0, A.mult)); V(tt(X, out, j2, A.add))
        V(tr(xt, X)); V(ts(mask, xt, 33793.0, A.is_le)); V(scan(sc, mask, xt, 33792.5, A.mult, A.max)); V(tr(k2, sc))
        V(ts(y2, k2, M34, A.add, M34 + 65536.0, A.subtract))
        if VIAPE:
            P([mm(i1, IF, half(EM, h), True, False), mm(i1, IS, y2, False, True)])
            V(ts(ix, i1, 16.0 * E - 1.0, A.min))
        else:
            V(ts(i1, y2, E / 2048.0, A.mult, cap, A.min)); V(tt(i2, i1, half(EM, h), A.add)); V(cp(ix, i2))
        ad = f("ad")
        S(act(ad, real, F.Identity, 65504.0, 27648.0 - 65504.0))
        S(act(BG[h], ind(WIN[d], ix), F.Copy))
        bx = pb(h, 3, 1, 1)
        Lm = f("Lm")
        P(group(Lp, [(IF, CT), (IF, k2), (NF, y2)]))
        if d == 0:
            V(ts(oP, Lp, -1184.0, A.add))
        V(tt(Lm, Lp, real, A.mult))
        P(group(bx, [(sel(EXT, k), sub(BG[h], k, WIDE, 16)) for k in range(16)]))
        if d == 0:
            V(ts(obb, y2, 1.0 / 2048, A.mult, m16, A.add))
        p2, p3 = T_("p2", h, i32, HW), T_("p3", h, i32, HW)
        V(tt(p1, bx, Lm, A.mult)); V(tt(p2, p1, ad, A.add))
        V(ts(p3, p2, 5, A.arith_shift_right, NW - 1, A.bitwise_and)); V(cp(oL, p3))
        return n

    def split(h, nm, src):
        pay = T_("pay" + nm, h, i32, W2)
        V([ts(half(pay, 0), src, 8, A.arith_shift_right), ts(half(pay, 1), src, 255, A.bitwise_and)])
        return pay

    def hot(d, names):
        hb, lh = T_("bhb", 0, b16, E), T_("blh", 0, h16, E)
        at = 0
        for x in names:
            V([ts(sub(hb, at, at + wid(x)), x, 1.0 / 128, A.mult, 128.50390625, A.add), ts(sub(lh, at, at + wid(x)), x, 0.0, A.add)])
            at += wid(x)
        ins = []
        for k in range(2):
            for o, a, b in ((lambda c, n: bank(6, c + k * n, n), 0, 128), (lambda c, n: part(bank(6, c + 2 * n, n), 64 * k, 64 * k + 64), 128, E)):
                ins += [mm(o(0, 128), sub(hb, a, b), ek(k))]
                ins += group(o(384, 8), [(sub(lh, a, b), sub(E8h, 8 * k, 8 * k + 8)), (sub(hb, a, b), sub(E8n, 8 * k, 8 * k + 8))])
        P(ins)
        S(act(sub(LOC, 24 * d, 24 * d + 24), bank(6, 384, 24), F.Identity, 16512.0))
        V(tt(sub(A0, 384 * d, 384 * d + 384), bank(6, 0, 384), HP, A.is_equal))
        for c in range(3):
            V([ts(sub(HOT, 128 * j, 128 * j + 128), IO, sub(LOC, j, j + 1), A.is_equal) for j in range(24 * d + 8 * c, 24 * d + 8 * c + 8)])

    def reduce(d, h, src, out):
        if d in RED:
            for c in range(0, 16, PCUT):
                P([mm(bank(RB[d], 0, HW), RF if d == 2 else IF, sub(src, k, WIDE, 16), k == 0, k == 15) for k in range(c, c + PCUT)])
            S(act(out, bank(RB[d], 0, HW), F.Copy))
            return
        b = sub(SCB, d * SW, (d + 1) * SW + 8)
        for c2 in range(2):
            V([scan(sub(b, 136 * c + 8, 136 * c + 136), sub(src, 256 * c, 256 * c + 256, 2), sub(src, 256 * c + 1, 256 * c + 256, 2),
                    0.0, A.add, A.add) for c in range(NC // 2 * c2, NC // 2 * (c2 + 1))])
        V(tt(out, sub(b, 15, SW + 8, 8), sub(b, 7, SW, 8), A.subtract))

    def fetch(out, win, lst, times=None, onv=False):
        n = HW // CUT
        for c in range(CUT):
            o, x = sub(out, 16 * n * c, 16 * n * (c + 1)), ind(win, sub(lst, n * c, n * (c + 1)))
            if onv:
                V(cp(o, x))
            elif times is None:
                S(act(o, x, F.Copy))
            else:
                V(tt(o, x, sub(times, 16 * n * c, 16 * n * (c + 1)), A.mult))

    def finish(t, D, Dn):
        for h in range(NP):
            yo, c0, bk = f32(HW), t * E + h * HW, bank(7, 0, HW)
            three = [D[0][h], Dn[0][h], Dn[1][h]]
            if len(RED) == 3:
                P(group(bk, [(IF, x) for x in three]))
                V(tt(yo, bk, sub(xv, c0, c0 + HW), A.mult))
            else:
                s1, s2 = T_("s1", h, f32, DW), T_("s2", h, f32, HW)
                a, b = [three[d] for d in range(3) if d not in RED], [three[d] for d in RED]
                if len(a) == 2:
                    V(tt(s1, a[0], a[1], A.add)); V(tt(s2, ind(s1, sub(YL, 0, NC)), b[0], A.add))
                    V(tt(yo, s2, sub(xv, c0, c0 + HW), A.mult))
                else:
                    V(tt(s2, ind(a[0], sub(YL, 0, NC)), b[0], A.add)); V(tt(bk, s2, b[1], A.add))
                    V(tt(yo, bk, sub(xv, c0, c0 + HW), A.mult))
            dma("Y", [(hbm("y", 0, 128, c0, c0 + HW), yo)], 2500, "outy")

    def update(t, WG):
        for d in range(3):
            e = E0R if d == 2 else ek(0)
            bk = bank(4 + d, 0, 384)
            P([mm(sub(bk, 0, 128), sub(WG[d], 0, 128), e), mm(sub(bk, 128, 256), sub(WG[d], 0, 128), e),
               mm(part(sub(bk, 256, 384), 0, 64), sub(WG[d], 128, E), e), mm(part(sub(bk, 256, 384), 64, 128), sub(WG[d], 128, E), e)])
            V(tt(sub(AW, 384 * d, 384 * d + 384), bk, sub(A0, 384 * d, 384 * d + 384), A.mult))
        ins = []
        for g in range(8):
            ins += group(bank(4, 16 * g, 16), [(sub(HOT, 128 * (8 * c + g), 128 * (8 * c + g) + 128), sub(AW, 128 * c + 16 * g, 128 * c + 16 * g + 16))
                                               for c in range(9)])
        P(ins)
        m1, m2 = T_("m1", 0, b16, 128), T_("m2", 0, b16, 128)
        V(ts(m1, bank(4, 0, 128), -0.5, A.max, 1.0, A.min))
        P(mm(bank(5, 0, 128), m1, I1))
        V(ts(m2, bank(5, 0, 128), 1.0, A.add))
        for c in range(4):
            bk = bank((6, 4, 5, 6)[c], 0, 512)
            P([mm(sub(bk, 128 * j, 128 * j + 128), ek(4 * c + j), m2) for j in range(4)])
            V(tt(sub(wU, 512 * c, 512 * c + 512), bk, sub(w, 512 * c, 512 * c + 512), A.mult))
        for c in range(2):
            V(ts(sub(w, 1024 * c, min(NW - 1, 1024 * c + 1024)), sub(wU, 1024 * c, min(NW - 1, 1024 * c + 1024)), 0.25, A.max, 4.0, A.min))
        products(t + 1)

    products(0)
    windows(0, 0); windows(0, 1)
    for t in range(EP):
        last = t == EP - 1
        PP = PT[t % 2]
        names = [sub(bn, t * E, (t + 1) * E), T_("nm", 1, i32, E)]
        WG = [b16(E), b16(E), b16(E)]
        votes, vall, n3all = f32(E), f32(E), u16(E)
        on, on2, onr = u16(5 * E), u16(5 * E), T_("onr", t % 2, u16, 4 * E)
        Da, Dna = [f32(E), f32(E)], [f32(E), f32(E)]
        D = [[T_("d1%d" % (t % 2), h, f32, HW) for h in range(NP)]] + [[half(x, h) for h in range(NP)] for x in Da]
        Dn = [[half(x, h) for h in range(NP)] for x in Dna]
        m12, m23 = [], []
        for h in range(NP):
            UP[0] = LEAD * (NP - 1 - h)
            lst = half(sub(L1, t * E, (t + 1) * E), h)
            ou, nu, nb = T_("ou%d" % t, h, u16, 4 * HW), sub(on, 4 * HW * h, 4 * HW * (h + 1)), T_("bb", h, b16, W2)
            pay = split(h, "1", half(names[0], h))
            cnt = strong(t, 0, h, lst)
            children(t, 0, h, cnt, half(ou, 3), pay, bb1, nl1, zz1, half(ou, 0), half(ou, 1), half(ou, 2))
            send([(ou, [(1, nu)])])
            m12.append((nu, nb, sub(onr, 4 * HW * h, 4 * HW * (h + 1))))
        if not last:
            windows(t + 1, 0)
            hot(0, [sub(L1, t * E, (t + 1) * E)])
        keep = []
        for h in range(NP):
            UP[0] = LEAD * (NP - 1 - h)
            nu, nb = m12[h][:2]
            nl, zz, st = T_("nl", h, b16, HW), T_("zz", h, b16, HW), T_("st2", h, b16, HW)
            V(cp(half(names[1], h), half(nu, 0)))
            pay = split(h, "2", half(names[1], h))
            V(ts(nb, sub(nu, W2, 2 * W2), 0.0, A.add))
            V([ts(nl, half(nb, 0), 25.0, A.max, 31.0, A.subtract), ts(zz, half(nb, 0), 31.0, A.is_ge, 0.5, A.add)])
            cnt = strong(t, 1, h, half(nu, 0))
            o3, n3, nc = u16(HW), half(n3all, h), b16(HW)
            keep.append(children(t, 1, h, cnt, st, pay, half(nb, 0), nl, zz, o3, None, None))
            oc = b16(HW)
            V(tt(oc, st, half(nb, 1), A.add))
            send([(o3, [(1, n3)]), (oc, [(1, nc)])])
            m23.append((n3, nc))
        if not last:
            windows(t + 1, 1)
            hot(1, [half(x[0], 0) for x in m12])
        en, ef, ko, kn = T_("en", 0, b16, E), T_("ef", 0, f32, E), sub(on, 4 * E, 5 * E), sub(on2, 4 * E, 5 * E)
        P([mm(half(bank(5, 0, E), h), TRI, keep[h]) for h in range(NP)])
        S(act(en, bank(5, 0, E), F.Copy))
        for c in range(4):
            ss = range(4 * c, 4 * c + 4)
            if t in THV:
                V([ts(sub(TH, s * E, (s + 1) * E), en, -float(s), A.is_ge, 0.5, A.subtract) for s in ss])
            else:
                S([act(sub(TH, s * E, (s + 1) * E), en, F.Sign, s + 0.5) for s in ss])
            P([mm(bank(5, E, E), sel(SELb if t in THV else SELq, s, 1), sub(TH, s * E, (s + 1) * E), s == 0, s == 15) for s in ss])
        V(tt(ef, bank(5, E, E), E16, A.add)); V(cp(ko, ef))
        send([(on, [(1, on2)])])
        n2 = sub(on2, 0, 4 * E)
        dma("Y", [(part(onr, 16, 128), part(n2, 0, 112)), (part(onr, 0, 16), part(n2, 112, 128))], 2400)
        for h in range(NP):
            UP[0] = LEAD * (NP - 1 - h)
            n3, nc = m23[h]
            st, vo = T_("st3", h, b16, HW), half(vall, h)
            cnt = strong(t, 2, h, n3)
            V(ts(st, cnt, 1.0, A.is_ge))
            vt = pb(h, 3, 1, 1)
            P(group(vt, [(BLK, nc), (UNROLL, st)]))
            if last:
                V(cp(vo, vt))
            else:
                vd = lambda j: sub(VDn, 2 * E * j + t * E + h * HW, 2 * E * j + t * E + (h + 1) * HW)
                po, pd = pb(h, 1), pb(h, 2)
                V(tt(po, vt, vd(0), A.is_ge)); V(cp(vo, vt)); V(tt(pd, po, vd(1), A.subtract)); V(tt(half(WG[2], h), pd, vd(2), A.mult))
        UP[0] = 0.0
        if not last:
            send([(WG[2], [(2, WG[0])]), (WG[2], [(3, WG[1])])])
            hot(2, [n3all])
        for h in range(NP):
            fetch(tv[0][h], PP, half(sub(L1, t * E, (t + 1) * E), h), None, (t, 0, h) in ONV)
            reduce(0, h, tv[0][h], D[0][h])
        if t:
            finish(*todo)
        for h in range(NP):
            nu = m12[h][0]
            fetch(av[h], ft, half(nu, 1))
            fetch(tv[1][h], PP, half(nu, 0), av[h])
            reduce(1, h, tv[1][h], D[1][h])
        if last:
            send([(Da[0], [(3, Dna[0])])])
        for h in range(NP):
            nr = m12[h][2]
            fetch(av[h], fR, half(nr, 1))
            fetch(sub(v2[h], 0, WIDE), fR, half(nr, 0), av[h])
            fetch(tv[0][h], PP, m23[h][0], None, (t, 2, h) in ONV)
            fetch(tv[1][h], v2[h], half(kn, h), tv[0][h])
            reduce(2, h, tv[1][h], D[2][h])
        send([(Da[1], [(2, Dna[1])]), (vall, [(2, votes)])] + ([] if last else [(Da[0], [(3, Dna[0])])]))
        dma("Y", [(hbm("cv", 0, 8, t * E, (t + 1) * E), part(votes, 0, 128, 16))], 2500, "outy")
        todo = (t, D, Dn)
        if not last:
            update(t, WG)
    finish(*todo)


def depend():
    seen = {}
    for i, o in enumerate(OPS):
        deps = set()
        for vs, wr in ((o["R"], False), (o["W"], True)):
            for v in vs:
                if v[0] not in ARENA and v[0][:2] != "ps":
                    continue
                ps = v[0][:2] == "ps"
                a, b = (0, 512) if ps else (v[4], v[5])
                for (j, a2, b2, w2) in seen.get(v[0], []):
                    if j != i and a < b2 and a2 < b and (wr or w2 or (ps and OPS[j]["q"] != o["q"])):
                        deps.add(j)
        for vs, wr in ((o["R"], False), (o["W"], True)):
            for v in vs:
                ps = v[0][:2] == "ps"
                a, b = (0, 512) if ps else (v[4], v[5])
                l = seen.setdefault(v[0], [])
                if wr and v[6] == 1 and (v[1], v[2], v[3]) == (0, 128, 1):
                    l[:] = [x for x in l if x[0] == i or not (a <= x[1] and x[2] <= b)]
                l.append((i, a, b, wr))
        o["deps"] = sorted(deps)


def schedule(slack=SLACK, same=60.0, other=110.0):
    n = len(OPS)
    kids = [[] for o in OPS]
    for i, o in enumerate(OPS):
        for j in o["deps"]:
            kids[j].append(i)
    pr = [0.0] * n
    for i in range(n - 1, -1, -1):
        pr[i] = OPS[i]["ns"] + OPS[i]["lat"] + max([pr[k] + other for k in kids[i]] + [0.0])
    for i in range(n - 1, -1, -1):
        pr[i] = max([pr[i] + OPS[i]["up"]] + [pr[k] + 1.0 for k in kids[i]])
    best = top = None
    rng = np.random.default_rng(SEED)
    for turn in range(TURNS):
        order = listing(pr, kids, slack, same, other)
        at, span = replay(order, same, other)
        if best is None or span < best[1] + HEAT * (1.0 - turn / TURNS):
            if best is None or span < top[1]:
                top = (order, span, at)
            best = (order, span, at, list(pr))
        pr = list(best[3])
        a = int(rng.integers(0, n))
        b = a + int(rng.integers(1, 40))
        c = float(rng.normal()) * MIX
        q = "VSP*"[int(rng.integers(0, 4))]
        for i in range(n - 1, -1, -1):
            move = c if a <= i < b and q in (OPS[i]["q"], "*") else 0.0
            pr[i] = max([pr[i] + move] + [pr[k] + 1.0 for k in kids[i]])
    best = top
    for i in range(n):
        OPS[i]["at"] = best[2][i]
    return best[0], best[1]


def listing(pr, kids, slack, same, other):
    n = len(OPS)
    fin, left = [None] * n, [len(o["deps"]) for o in OPS]
    free, order = {q: 0.0 for q in "VSPGY"}, {q: [] for q in "VSPGY"}
    pool = set(i for i in range(n) if left[i] == 0)
    for step in range(n):
        est, front = {}, sorted(pool)
        for i in front:
            o = OPS[i]
            est[i] = max([o["late"], free[o["q"]]] + [fin[j] + (same if OPS[j]["q"] == o["q"] else other) for j in o["deps"]])
        end = min(est.values()) + SIGHT
        while front:
            more = []
            for i in front:
                if est[i] + OPS[i]["ns"] + OPS[i]["lat"] < end:
                    for k in kids[i]:
                        if k not in est and all(fin[j] is not None or j in est for j in OPS[k]["deps"]):
                            o = OPS[k]
                            est[k] = max([o["late"], free[o["q"]]] + [(fin[j] if fin[j] is not None else est[j] + OPS[j]["ns"] + OPS[j]["lat"])
                                                                      + (same if OPS[j]["q"] == o["q"] else other) for j in o["deps"]])
                            more.append(k)
            front = more
        best = None
        for c in pool:
            q, e = OPS[c]["q"], est[c] + OPS[c]["ns"]
            held = any(pr[i] > pr[c] + GAP and OPS[i]["q"] == q and est[i] + slack < e for i in est)
            key = (held, est[c] // GRAIN, -pr[c], c)
            if best is None or key < best:
                best = key
        c = best[3]
        q = OPS[c]["q"]
        pool.remove(c)
        order[q].append(c)
        free[q] = est[c] + OPS[c]["ns"]
        fin[c] = free[q] + OPS[c]["lat"]
        for k in kids[c]:
            left[k] -= 1
            if left[k] == 0:
                pool.add(k)
    return order


def replay(order, same, other):
    fin, at, free, pos = {}, [0.0] * len(OPS), {q: 0.0 for q in order}, {q: 0 for q in order}
    go = True
    while go:
        go = False
        for q in order:
            while pos[q] < len(order[q]):
                i = order[q][pos[q]]
                o = OPS[i]
                if any(j not in fin for j in o["deps"]):
                    break
                at[i] = max([free[q]] + [fin[j] + (same if OPS[j]["q"] == q else other) for j in o["deps"]])
                free[q] = at[i] + o["ns"]
                fin[i] = free[q] + o["lat"]
                pos[q] += 1
                go = True
    return at, (max(fin.values()) if len(fin) == len(OPS) else 1e18)


plan()
depend()
ORDER, SPAN = schedule()
SCRATCH = {a: ("sbuf", [128, TOP[a]], ARENA[a]) for a in ARENA}
for _b in range(8):
    SCRATCH["ps%d" % _b] = ("psum", [128, 512], "float32")
SEMAPHORES = list(SEMS)


def deal(lanes, n):
    out = []
    for j in range(n - 1):
        out.append(lanes[:len(lanes) // 2])
        lanes = lanes[len(lanes) // 2:]
    return out + [lanes]


def rank_program(g, core, T, topo):
    rank = T.rank_of(core)
    if rank is None:
        return
    cores = list(T.cores)
    n = len(cores)
    lanes = [e for e in range(16) if all(e in topo.engines(a, b) for a in cores for b in cores if a != b)]
    eng = {"V": g.vector, "S": g.scalar, "P": g.tensor, "G": g, "Y": g.sync}
    mark, total = {}, {}
    for q in ORDER:
        for i in ORDER[q]:
            o = OPS[i]
            if o["kind"] == "c":
                s, k = "c" + q, len(o["ins"])
            elif o["kind"] == "d":
                s, k = o["sem"], 16 * len(o["ins"])
            else:
                cut = deal(lanes, len(o["x"]))
                s, k = o["sem"], sum(len(c) * len(x[1]) for c, x in zip(cut, o["x"]))
                total["sent"] = total.get("sent", 0) + sum(len(c) for c in cut)
            total[s] = total.get(s, 0) + k
            mark[i] = (s, total[s])
    waited = {}
    for q in ORDER:
        e, have = eng[q], {}
        for i in ORDER[q]:
            o = OPS[i]
            need = {}
            for j in o["deps"]:
                s, k = mark[j]
                if not (q == "P" and s == "cP"):
                    need[s] = max(need.get(s, 0), k)
            for s in need:
                if need[s] > have.get(s, 0):
                    e.wait_ge(T.sem[s], need[s])
                    have[s] = need[s]
                    waited[s] = max(waited.get(s, 0), need[s])
            if o["kind"] == "r":
                cut = deal(lanes, len(o["x"]))
                trs = []
                for j, (src, dsts) in enumerate(o["x"]):
                    ids = [topo.addr(cores[(rank + k) % n], core) for k, l in dsts]
                    trs.append(RemoteDMATransfer(dst_ids=[DstId(rid=a, pnc=b) for a, b in ids],
                                                 dma_engine_mask=sum(1 << x for x in cut[j]),
                                                 remote_sem=T.sem[o["sem"]], srcs=[ap(T, src)], dsts=[ap(T, l) for k, l in dsts]))
                g.remote_dma_fused(trs, local_sem=T.sem["sent"])
                continue
            for name, args, kw, r, w_, ns in o["ins"]:
                x = [ap(T, v) for v in args]
                kk = {k: ap(T, kw[k]) for k in kw}
                done = call(e, name, x, kk)
                done.then_inc(T.sem[mark[i][0]], 16 if o["kind"] == "d" else 1)
    for s in total:
        if total[s] > waited.get(s, 0):
            g.wait_ge(T.sem[s], total[s])


def call(e, name, x, kk):
    if name == "tensor_tensor":
        return e.tensor_tensor(*x)
    if name == "tensor_scalar":
        return e.tensor_scalar(*x)
    if name == "tensor_copy":
        return e.tensor_copy(*x)
    if name == "transpose":
        return e.transpose(*x)
    if name == "tensor_tensor_scan":
        return e.tensor_tensor_scan(*x)
    if name == "memset":
        return e.memset(*x)
    if name == "activation":
        return e.activation(*x, **kk)
    if name == "matmul":
        return e.matmul(*x)
    if name == "iota":
        return e.iota(*x, **kk)
    if name == "affine_select":
        return e.affine_select(*x)
    return e.dma_start(*x)
